import numpy as np, ml_dtypes
CORES = [6,15,38,47]
N = 4
import mx_ref
BF = ml_dtypes.bfloat16
def gcols(t, e):
    v = np.concatenate([t.reshape(8, 16, -1, 4), np.zeros((8, 16, 1, 4), BF)], axis=2)
    return np.ascontiguousarray(np.stack([v[g][:, e[g]] for g in range(8)])).reshape(128, -1)
def tile(rs):
    return np.stack(rs, axis=2).reshape(128, -1).astype(BF)
def pick(q, e):
    c = np.concatenate([q[0].reshape(128, -1, 4), np.zeros((128, 1, 4), np.uint8)], axis=1); s = np.concatenate([q[1], np.ones((16, 1), np.uint8)], axis=1)
    return (np.ascontiguousarray(c[:, e].reshape(128, -1)), np.ascontiguousarray(s[:, e]))
def join(*qs):
    return (np.concatenate([q[0] for q in qs], axis=1), np.concatenate([q[1] for q in qs], axis=1))
def put(q, e, v):
    c, s = q[0].reshape(128, -1, 4).copy(), q[1].copy(); c[:, e] = v[0].reshape(128, -1, 4); s[:, e] = v[1]
    return (c.reshape(128, -1), s)
def pk(c, s):
    return (np.ascontiguousarray(c), mx_ref.live(s))
def emit(q):
    return q[0], q[1]
def packed(v, rng):
    q = [mx_ref.quantize(np.ascontiguousarray(v[r])) for r in range(N)]
    return np.stack([a for a, b in q]), np.stack([mx_ref.plane(b, rng) for a, b in q])
def values_of_codes():
    e, c = np.zeros((128, 128, 4), np.float32), np.zeros((128, 2, 4), np.uint8)
    e[np.arange(128), np.arange(128), 0] = 1
    c[:127, :, 0] = np.arange(256).reshape(2, 128).T[:127]
    return mx_ref.matmul(mx_ref.quantize(e.reshape(128, 512).astype(BF)), (c.reshape(128, 8), np.full((16, 2), 127, np.uint8))).T.reshape(-1).astype(np.float64)
CODE_VALUE, SCALE_VALUE = values_of_codes(), 2.0 ** (np.arange(256) - 127.0)
def decode(q):
    return (CODE_VALUE[q[0]].reshape(16, 8, -1, 4) * SCALE_VALUE[q[1]][:, None, :, None] + 0.0).reshape(128, -1).astype(np.float32)
def f(rng, *shape):
    return mx_ref.flush((rng.standard_normal(shape, dtype=np.float32) * np.exp2(rng.integers(-2, 3, shape[:-1] + (1,)))).astype(BF))
def wide(rng, *shape, cols=0):
    v = rng.standard_normal(shape, dtype=np.float32) * np.exp2(rng.integers(-12, 13, shape)).astype(np.float32)
    if cols: v *= np.repeat(np.exp2(rng.integers(-cols, cols + 1, shape[:-2] + (1, shape[-1] // 4))) * (rng.random(shape[:-2] + (1, shape[-1] // 4)) > 0.0625), 4, axis=-1).astype(np.float32)
    return mx_ref.flush(v.astype(BF))
C, K, DEP, R = 320, 160, 40, 3
SOURCE = [7, 0, 1, 1, 2, 2, 3, 3]
LEVEL = [0, 1, 2, 2, 3, 3, 3, 3]
ITEM = 8 * (np.arange(C) % DEP) + np.arange(C) // DEP
def big(v):
    v = v.astype(np.float32)
    v[np.abs(v) < np.float32(2.0 ** -16)] = 0
    return v.astype(BF)
def numbers_of(rng):
    return {"x": big(f(rng, N, 128, 4 * C)), "u": np.array(f(rng, N, 128, 512)), "v": np.array(f(rng, N, 128, 512))}
def layers(rng):
    return big(f(rng, N, 128, 2048).astype(np.float32) * np.float32(0.5)).reshape(N, 8, 16, 4, 8, 16, 4)
def weights(rng, w):
    c, p = packed(np.ascontiguousarray(w).reshape(N, 128, 2048), rng)
    return {"wc": c, "ws": p}
def own_bits(u):
    for b in range(3): u[:, :, b::16] = 0
    for h in range(0, 128, 16):
        for b in range(3): u[:, h, h + b, b] = 1
def setup_inputs(rng):
    return {**numbers_of(rng), **weights(rng, layers(rng))}
def setup_inputs_ties(rng):
    d = numbers_of(rng)
    e = rng.permutation(N)
    k = rng.integers(-1, 2, (N, 8, C, 3)).astype(np.float32)
    k[e[0]] = 0
    k[e[1]] = 1
    for g in range(8): k[e[2], g, :, 0] = 2.0 * (LEVEL[g] % 2) - 1.0
    x = d["x"].reshape(N, 8, 16, C, 4)
    x[:, :, :8] = 0
    x[:, :, 0, :, :3] = k.astype(BF)
    u = d["u"].reshape(N, 128, 128, 4)
    own_bits(u)
    w = layers(rng)
    w[:, :, :, :, :, :8] = 0
    return {"x": x.reshape(N, 128, 4 * C), "u": u.reshape(N, 128, 512), "v": d["v"], **weights(rng, w)}
def setup_inputs_near(rng):
    d = numbers_of(rng)
    x = d["x"].reshape(N, 8, 16, C, 4)
    u = d["u"].reshape(N, 128, 128, 4)
    o = rng.permutation(N) % 4
    x[:, :, :8] = 0
    for b in range(3): u[:, :, b::16] = 0
    for r in range(N):
        a = rng.integers(-1, 2, (8, C, 3)).astype(np.float32)
        b = np.where(rng.random((8, C, 3)) < 0.75, -a, rng.integers(-1, 2, (8, C, 3))).astype(np.float32)
        k = np.float32(2.0 ** -27 if o[r] < 2 else 1.0)
        a, b = a * k, b * k
        for g in rng.permutation(8)[:4]: a[g, rng.integers(C)] = 2.0 ** 18 * rng.choice([-1.0, 1.0], 3)
        x[r, :, 0, :, :3] = a.astype(BF)
        x[r, :, 1, :, :3] = b.astype(BF)
        m = 2.0 ** -30 if o[r] % 2 == 0 else 1.0
        for h in range(0, 128, 16):
            for t in range(3):
                u[r, h, h + t, t] = 1.125 * m
                u[r, h + 1, h + t, t] = m
    w = layers(rng)
    w[:, :, :8] = 0
    w[:, :, :, :, :, :8] = 0
    return {"x": x.reshape(N, 128, 4 * C), "u": u.reshape(N, 128, 512), "v": d["v"], **weights(rng, w)}
def setup_inputs_late(rng):
    d = numbers_of(rng)
    s = rng.integers(6, 8, (N, 8, 8, DEP))
    for g in range(8):
        if g: s[:, g, :, 0] = LEVEL[g] - 1
        s[:, g, :, -1] = LEVEL[g]
    s[:, 7, 7] = 0
    s[:, 7, 7, -1] = 2
    e = int(rng.integers(N))
    s[e] = 7
    for g in range(8):
        if LEVEL[g] > 0: s[e, g, :, 0] = 7 - LEVEL[g]
        if LEVEL[g] < 3: s[e, g, :, -1] = 6 - LEVEL[g]
    s[e, 2:4, :7, -1] = 2
    for h in (0, 1, 6, 7):
        s[e, 4:, h, 0] = 2
        s[e, 4:, h, 1] = 3
    s[e, 4:, 5, 1] = 6
    s = s.reshape(N, 8, C)
    x = d["x"].reshape(N, 8, 16, C, 4)
    x[:, :, :8] = 0
    x[:, :, 0, :, :3] = (2.0 * ((s[..., None] >> np.array([2, 1, 0])) & 1) - 1.0).astype(np.float32).astype(BF)
    k = (1.0 + (2 * rng.integers(0, 64, (N, 8, 8, C, 4)) + 1) / 128.0) * np.exp2(-1.0 * rng.integers(8, 15, (N, 8, 8, C, 4))) * rng.choice([-1.0, 1.0], (N, 8, 8, C, 4))
    k[:, :, 0, :, 0] = 1.96875
    x[:, :, 8:] = k.astype(np.float32).astype(BF)
    u = d["u"].reshape(N, 128, 128, 4)
    own_bits(u)
    w = layers(rng)
    w[:, :, :, :, :, :8] = 0
    return {"x": x.reshape(N, 128, 4 * C), "u": u.reshape(N, 128, 512), "v": d["v"], **weights(rng, w)}
def setup_inputs_ends(rng):
    o = rng.permutation(N)
    x = rng.choice([-1.0, 1.0], (N, 8, 1, C, 1)) * np.ones((1, 1, 16, 1, 4))
    u, v = rng.choice([-1.0, 1.0], (N, 128, 512)), rng.choice([-1.0, 1.0], (N, 128, 512))
    w = np.zeros((N, 128, 2048), np.float32)
    for r in range(N):
        if o[r] == 0: x[r] = 1.0
        if o[r] == 3: x[r] = -1.0
        if o[r] in (0, 3): u[r] = 1.0
        x[r] *= 2.0 ** 19 if o[r] % 2 == 0 else 2.0 ** -27
        u[r] *= 2.0 ** 30 if o[r] % 4 < 2 else 2.0 ** -30
        v[r] *= 2.0 ** 30 if o[r] % 4 in (0, 3) else 2.0 ** -30
        w[r] = (2.0, -2.0, 0.0)[o[r] % 3]
    return {"x": x.astype(np.float32).reshape(N, 128, 4 * C).astype(BF), "u": u.astype(np.float32).astype(BF), "v": v.astype(np.float32).astype(BF), **weights(rng, w.astype(BF))}
def setup_inputs_spread(rng):
    d = setup_inputs(rng)
    d["x"] = big(wide(rng, N, 128, 4 * C, cols=3))
    return d
def check_inputs(d):
    b = []
    for k, m in (("x", 2.0 ** 19), ("u", 2.0 ** 30), ("v", 2.0 ** 30)):
        a = np.abs(d[k].astype(np.float32))
        if not (np.isfinite(a).all() and ((a == 0) | (a >= 2.0 ** -30) & (a <= m)).all()): b.append("a value of " + k)
    none, least, most = [emit(mx_ref.quantize(np.full((128, 16), k, np.float32).astype(BF)))[1][0, 0] for k in (0.0, 2.0 ** -30, 2.0 ** 30)]
    for r in range(N):
        if ((d["wc"][r] == 0x7F) | (d["wc"][r] == 0xFF)).any(): b.append("wc: a code that is no number")
        s = mx_ref.live(d["ws"][r])
        if ((s != none) & ((s < least) | (s > most))).any(): b.append("ws: a scale out of range")
        a = np.abs(decode(pk(d["wc"][r], d["ws"][r])).astype(np.float64)).reshape(128, 512, 4)
        if not (np.sum(a, axis=(0, 2)) <= 1024).all(): b.append("W: a column that adds up to more than 1024")
    return b
def times(sym, wait):
    sym, wait = sym.reshape(8, DEP), wait.reshape(8, DEP)
    t, last = np.zeros((8, DEP), np.int64), np.zeros(8, np.int64)
    for i in range(DEP):
        last = np.maximum(last, wait[:, i]) + (1 + sym[:, i])
        t[:, i] = last
    return t.reshape(C)
def orders(sym):
    o, b = np.zeros((8, C), np.int64), np.zeros((8, K), np.int64)
    first, least = np.full((8, 8), -1), np.zeros((8, 8), np.int64)
    for g in range(8):
        e = SOURCE[g]
        t = times(sym[g], least[e][sym[g]] if g > 0 else np.zeros(C, np.int64))
        o[g] = np.argsort(t, kind="stable")
        for s in range(8):
            p = np.flatnonzero(sym[g][o[g]] == s)
            if len(p) > 0:
                first[g, s] = o[g, p[0]]
                least[g, s] = t[o[g, p[0]]]
        l = o[g, :K]
        p = first[e][sym[g][l]] if g > 0 else l
        b[g] = np.where(p < 0, l, p)
    return o, b
def reference(x, u, v, wc, ws):
    qu = [mx_ref.quantize(u[r]) for r in range(N)]
    lay = [pk(wc[r], ws[r]) for r in range(N)]
    now = [x[r] for r in range(N)]
    order = np.zeros((N, 8, C), np.int64)
    for t in range(R):
        stay, sent = [], []
        for r in range(N):
            q = mx_ref.quantize(now[r])
            full = decode(q)
            s = mx_ref.matmul(qu[r], q)
            order[r], mate = orders(4 * (s[::16] > 0) + 2 * (s[1::16] > 0) + (s[2::16] > 0))
            a = full.reshape(8, 16, C, 4)
            z = np.stack([(a[g][:, order[r, g, :K]] + a[SOURCE[g]][:, mate[g]]) * np.float32(0.5) for g in range(8)])
            sent.append(mx_ref.quantize(np.ascontiguousarray(z.reshape(128, 4 * K).astype(BF))))
            stay.append(gcols(full.astype(BF), order[r][:, K:]))
        for r in range(N):
            q = sent[r - 1]
            d = decode(q)
            h = tile([mx_ref.matmul(pick(lay[r], np.arange(128 * b, 128 * b + 128)), q) * np.float32(0.0078125) + d[:, b::4] for b in range(4)])
            items = np.concatenate([stay[r], h], axis=1).reshape(128, C, 4)
            now[r] = np.ascontiguousarray(items[:, ITEM].reshape(128, 4 * C))
    y, op = np.zeros((N, 128, C), np.float32), np.zeros((N, 8, C), np.float32)
    oc, osc = np.zeros((N, 128, 4 * C), np.uint8), np.zeros((N, 16, C), np.uint8)
    for r in range(N):
        q = mx_ref.quantize(now[r])
        y[r] = mx_ref.matmul(mx_ref.quantize(v[r]), q)
        op[r] = order[r]
        oc[r], osc[r] = emit(q)
    return {"y": y, "op": op, "oc": oc, "osc": osc}

@@ -1,0 +1,529 @@
+from concourse.mybir import dt, AluOpType as O, AxisListType, ActivationFunctionType as AF
+
+NS = 11
+NV = 20 - NS
+HUGE = 1.0e25
+BIG = float(2 ** 20)
+F4 = "float8_e4m3fn_x4"
+
+
+def _decl():
+    d = {}
+
+    def sb(names, n, t):
+        for k in names.split():
+            d[k] = ("sbuf", [128, n], t)
+    sb("xt fp f2", 1280, "bfloat16")
+    sb("xk xh zt pz sj", 640, "bfloat16")
+    sb("uv", 1024, "bfloat16")
+    sb("zz", 512, "bfloat16")
+    sb("ct et", 2048, "bfloat16")
+    sb("fl", 1408, "bfloat16")
+    sb("fab", 960, "bfloat16")
+    sb("scn", 160 * NV, "bfloat16")
+    sb("idx", 256, "bfloat16")
+    for k, n in (("u", 128), ("up", 128), ("v", 128), ("w", 512), ("e", 512), ("h", 512), ("g", 512), ("a", 512), ("b", 512), ("c", 512), ("f", 352), ("n", 320)):
+        d["q" + k] = ("sbuf", [128, n], F4)
+        d["s" + k + "_p"] = ("sbuf", [128, n], "uint8")
+    for r in range(4):
+        d["q%d" % r] = ("sbuf", [128, 320], F4)
+        d["s%d_p" % r] = ("sbuf", [128, 320], "uint8")
+    for r in range(3):
+        for k in ("z", "l"):
+            d["q%s%d" % (k, r)] = ("sbuf", [128, 160], F4)
+            d["s%s%d_p" % (k, r)] = ("sbuf", [128, 160], "uint8")
+    sb("tg", 1536, "float32")
+    sb("par th hrow si0 si1 ccol d0o dow vrow yo oprow tlo", 320, "float32")
+    sb("c0 d0h tt vv dst0 dst1 dst2 ast0 ast1 ast2 tl", 160, "float32")
+    sb("ix", 256, "float32")
+    sb("kap", 352, "float32")
+    sb("kt", 672, "float32")
+    sb("ex", 48, "float32")
+    sb("my acc", 20, "float32")
+    sb("win tw", 640, "float32")
+    sb("mcol", 8, "float32")
+    sb("ones mb tb", 32, "float32")
+    sb("cf", 64, "float32")
+    sb("ci mi wt w8 ft ub", 16, "int32")
+    sb("fx lx rx", 128, "int32")
+    sb("nx", 64, "int32")
+    sb("off12 offd offs offo nat", 32, "uint16")
+    sb("ll bl kl ulist", 16, "uint16")
+    sb("ku", 320, "uint16")
+    for b in range(8):
+        d["pb%d" % b] = ("psum", [128, 512], "float32")
+    return d
+
+
+SCRATCH = _decl()
+SEMAPHORES = ["sV", "sS", "sP", "sG", "dx", "du", "dw", "dws", "dv", "arr0", "arr1", "arr2", "loc", "doy", "doa"]
+
+
+def rank_program(g, core, T, topo):
+    rank = T.rank_of(core)
+    if rank is None:
+        return
+    nxt = T.cores[(rank + 1) % len(T.cores)]
+    queue = {"V": g.vector, "S": g.scalar, "P": g.tensor, "G": g, "Y": g.sync}
+    own = {"V": "sV", "S": "sS", "P": "sP", "G": "sG"}
+    count = {}
+    clock = {}
+    known = {k: {} for k in queue}
+    hist = {}
+
+    def norm(a):
+        if isinstance(a, str):
+            a = (a, 0, 1 << 20)
+        if a[0][:2] == "pb":
+            return (a[0], 0, 1 << 20)
+        return a
+
+    def accesses(reads, writes):
+        r = [norm(a) for a in reads]
+        return [(a, "p" if a[0][:2] == "pb" else "r") for a in r] + [(norm(a), "w") for a in writes]
+
+    def waits(q, acc):
+        need = {}
+        for (b, lo, hi), kind in acc:
+            for e in hist.get(b, []):
+                if e[0] >= hi or e[1] <= lo or (kind == "r" and e[2] == "r"):
+                    continue
+                if b[:2] == "pb" and kind == ("w" if e[2] == "w" else "p") and own.get(q) == e[3]:
+                    continue
+                need[e[3]] = max(need.get(e[3], 0), e[4])
+        kn = known[q]
+        for s in sorted(need, key=lambda s: -need[s]):
+            if kn.get(s, 0) >= need[s]:
+                continue
+            queue[q].wait_ge(T.sem[s], need[s])
+            for k, v in clock.get((s, need[s]), {}).items():
+                kn[k] = max(kn.get(k, 0), v)
+            kn[s] = max(kn.get(s, 0), need[s])
+
+    def record(q, sem, n, acc):
+        count[sem] = count.get(sem, 0) + n
+        v = count[sem]
+        clock[(sem, v)] = dict(known[q])
+        for (b, lo, hi), kind in acc:
+            h = hist.setdefault(b, [])
+            if kind == "r":
+                h[:] = [e for e in h if not (e[2] == "r" and e[3] == sem and e[0] >= lo and e[1] <= hi)]
+            else:
+                h[:] = [e for e in h if not (e[0] >= lo and e[1] <= hi)]
+            h.append([lo, hi, kind, sem, v])
+
+    def op(q, call, reads, writes):
+        acc = accesses(reads, writes)
+        waits(q, acc)
+        call(queue[q]).then_inc(T.sem[own[q]], 1)
+        record(q, own[q], 1, acc)
+
+    def dma(q, out, in_, reads, writes, sem):
+        acc = accesses(reads, writes)
+        waits(q, acc)
+        queue[q].dma_start(out, in_).then_inc(T.sem[sem], 16)
+        record(q, sem, 16, acc)
+
+    def V(call, reads, writes):
+        op("V", call, reads, writes)
+
+    def ts(out, in0, s1, s2, o0, o1, reads, writes):
+        if o1 is None:
+            V(lambda v: v.tensor_scalar(out, in0, s1, None, o0), reads, writes)
+        else:
+            V(lambda v: v.tensor_scalar(out, in0, s1, s2, o0, o1), reads, writes)
+
+    def tt(out, a, b, o, reads, writes):
+        V(lambda v: v.tensor_tensor(out, a, b, o), reads, writes)
+
+    def fill(out, val, writes):
+        V(lambda v: v.memset(out, val), [], writes)
+
+    def act(out, in_, f, reads, writes, **kw):
+        op("S", lambda s: s.activation(out, in_, f, **kw), reads, writes)
+
+    def iota(out, pat, base, cm, writes, f=True):
+        if f:
+            op("G", lambda e: e.iota(out, pat, base, cm, allow_small_or_imprecise_dtypes=True), [], writes)
+        else:
+            op("G", lambda e: e.iota(out, pat, base, cm), [], writes)
+
+    def quant(k, a, b, tile, lo, hi):
+        qn, sn = "q" + k, "s" + k + "_p"
+        V(lambda v: v.quantize_mx(T[qn][:, a:b], T[sn][:, a:b], T[tile][:, lo:hi]), [(tile, lo, hi)], [(qn, a, b), (sn, a, b)])
+
+    def mm(bank, n, k, a, m, b, start=True, stop=True):
+        qa, sa, qb, sq = "q" + k, "s" + k + "_p", "q" + m, "s" + m + "_p"
+        op("P", lambda t: t.matmul_mx(T["pb%d" % bank][:, 0:n], T[qa][:, a:a + 128], T[sa][:, a:a + 128], T[qb][:, b:b + n], T[sq][:, b:b + n], start, stop),
+           [(qa, a, a + 128), (sa, a, a + 128), (qb, b, b + n), (sq, b, b + n)], ["pb%d" % bank])
+
+    def between(todo):
+        if todo:
+            todo.pop(0)()
+
+    dma("Y", T.xt[:], T.x[:], [], ["xt"], "dx")
+    dma("S", T.uv[:, 0:512], T.u[:], [], [("uv", 0, 512)], "du")
+    dma("Y", T.qw[:].bitcast(dt.uint8), T.wc[:], [], ["qw"], "dw")
+    dma("Y", T["sw_p"][:], T.ws[:], [], ["sw_p"], "dws")
+    dma("Y", T.uv[:, 512:1024], T.v[:], [], [("uv", 512, 1024)], "dv")
+
+    fill(T.zz[:], 0.0, ["zz"])
+    fill(T.tg[:, 256:512], -1.0, [("tg", 256, 512)])
+    iota(T.ci[:, 0:1], [[1, 1]], 0, 1, [("ci", 0, 1)], f=False)
+    iota(T.ub[:, 0:8], [[16, 8]], 0, 0, ["ub"], f=False)
+    iota(T.par[:], [[0, 10], [1, 2], [0, 16]], 0, 0, ["par"])
+    iota(T.tg[:, 0:128], [[0, 4], [100, 2], [0, 16]], 0, 0, [("tg", 0, 128)])
+    iota(T.tg[:, 128:256], [[0, 4], [100, 2], [0, 16]], -100, 0, [("tg", 128, 256)])
+    for base, jj, code in ((256, 0, 8), (384, 1, 16)):
+        iota(T.tg[:, base + jj:base + 128:32], [[1, 2], [0, 2]], code, 0, [("tg", base, base + 64)])
+        iota(T.tg[:, base + jj + 2:base + 128:32], [[1, 4]], code, 0, [("tg", base + 64, base + 128)])
+    iota(T.c0[:], [[64, 4], [1, 40]], -1, 0, ["c0"])
+    for h in range(2):
+        for k in range(2):
+            lo = 512 + 128 * h + 64 * k
+            iota(T.tg[:, lo:lo + 64], [[0, 2], [100, 2], [0, 16]], k - 100 * h, 0, [("tg", lo, lo + 64)])
+    for h in range(2):
+        lo = 768 + 128 * h
+        iota(T.tg[:, lo:lo + 128], [[1, 4], [100, 2], [0, 16]], -100 * h, 0, [("tg", lo, lo + 128)])
+    iota(T.tg[:, 1024:1152], [[1, 8], [0, 16]], 0, 0, [("tg", 1024, 1152)])
+    fill(T.tg[:, 1152:1536], -1.0, [("tg", 1152, 1536)])
+    for i, (base, jj, code) in enumerate(((1152, 0, 8), (1152, 1, 17), (1280, 0, 9), (1408, 1, 16))):
+        iota(T.tg[:, base + jj:base + 128:32], [[2, 4]], code, 0, [("tg", 1152 + 96 * i, 1248 + 96 * i)])
+    iota(T.ix[:, 0:128], [[1, 128]], 0, 0, [("ix", 0, 128)])
+    iota(T.ix[:, 128:256], [[16, 4], [0, 2], [1, 16]], 0, 0, [("ix", 128, 256)])
+    iota(T.ix[:, 128:144], [[1, 16]], 112, 0, [("ix", 128, 256)])
+    iota(T.hrow[:], [[1, 8], [0, 40]], 0, 0, ["hrow"])
+    iota(T.si0[:], [[1, 320]], 1, 0, ["si0"])
+    iota(T.si1[:], [[1, 8], [8, 40]], 1, 0, ["si1"])
+    iota(T.ccol[:], [[1, 320]], 0, 0, ["ccol"])
+    iota(T.nx[:, 0:20], [[16, 20]], 0, 0, [("nx", 0, 20)], f=False)
+    for n, w in (("ct", 512), ("fl", 352)):
+        for b in range(4):
+            act(T[n][:, w * b:w * b + w], T.zz[:, 0:w], AF.Copy, ["zz"], [(n, w * b, w * b + w)])
+
+    def ci(i):
+        return T.ci[:, i:i + 1]
+
+    def cf(i):
+        return T.cf[:, i:i + 1]
+
+    def C(i):
+        return ("ci", i, i + 1)
+
+    def K(i):
+        return ("cf", i, i + 1)
+    RK, SG, HF, BK, GR = 1, 2, 3, 4, 5
+    ts(ci(RK), ci(0), 15, None, O.bitwise_and, None, [C(0)], [C(RK)])
+    ts(ci(GR), ci(0), 4, None, O.arith_shift_right, None, [C(0)], [C(GR)])
+    ts(ci(SG), ci(0), 7, None, O.bitwise_and, None, [C(0)], [C(SG)])
+    ts(ci(HF), ci(0), 16, 4, O.bitwise_and, O.arith_shift_right, [C(0)], [C(HF)])
+    ts(ci(BK), ci(0), 5, None, O.arith_shift_right, None, [C(0)], [C(BK)])
+    ts(cf(0), ci(RK), 3.0, None, O.is_ge, None, [C(RK)], [K(0)])
+    ts(cf(1), ci(RK), 6.0, None, O.is_ge, None, [C(RK)], [K(1)])
+    ts(cf(9), ci(RK), 9.0, 100.0, O.is_ge, O.mult, [C(RK)], [K(9)])
+    tt(cf(2), cf(0), cf(1), O.add, [K(0), K(1)], [K(2)])
+    tt(cf(10), cf(9), ci(GR), O.add, [K(9), C(GR)], [K(10)])
+    ts(cf(3), cf(2), -3.0, None, O.mult, None, [K(2)], [K(3)])
+    ts(cf(8), cf(2), 8.0, None, O.mult, None, [K(2)], [K(8)])
+    ts(cf(13), cf(2), 2.0, HUGE, O.is_equal, O.mult, [K(2)], [K(13)])
+    ts(cf(12), cf(2), 1.0, HUGE, O.is_equal, O.mult, [K(2)], [K(12)])
+    tt(cf(4), cf(3), ci(RK), O.add, [K(3), C(RK)], [K(4)])
+    tt(cf(11), cf(8), cf(10), O.add, [K(8), K(10)], [K(11)])
+    tt(cf(14), cf(12), cf(13), O.subtract, [K(12), K(13)], [K(14)])
+    ts(cf(5), cf(4), 1.0, 1.0, O.is_equal, O.add, [K(4)], [K(5)])
+    ts(cf(6), cf(4), 0.0, 3.0, O.is_equal, O.mult, [K(4)], [K(6)])
+    ts(T.ulist[:, 0:8], T.ub[:, 0:8], cf(4), None, O.add, None, ["ub", K(4)], ["ulist"])
+    tt(cf(7), cf(5), cf(6), O.add, [K(5), K(6)], [K(7)])
+    act(T.th[:], T.par[:], AF.Identity, ["par", K(14), K(13)], ["th"], scale=cf(14), bias=cf(13))
+    for b in range(4):
+        act(T.et[:, 512 * b:512 * b + 512], T.zz[:], AF.Copy, ["zz"], [("et", 512 * b, 512 * b + 512)])
+    ts(cf(20), ci(SG), -BIG, None, O.mult, None, [C(SG)], [K(20)])
+    ts(cf(21), ci(HF), 256.0, None, O.mult, None, [C(HF)], [K(21)])
+    ts(cf(22), ci(HF), 16.0, None, O.mult, None, [C(HF)], [K(22)])
+    ts(cf(23), ci(HF), 0.0, None, O.is_equal, None, [C(HF)], [K(23)])
+    ts(cf(24), ci(HF), 1.0, None, O.is_equal, None, [C(HF)], [K(24)])
+    for i, (src, least) in enumerate(((BK, 2.0), (BK, 1.0), (GR, 1.0))):
+        ts(cf(25 + 2 * i), ci(src), least, None, O.is_ge, None, [C(src)], [K(25 + 2 * i)])
+        ts(cf(26 + 2 * i), ci(src), least, 8.0, O.is_lt, O.mult, [C(src)], [K(26 + 2 * i)])
+    fill(T.ones[:], 1.0, ["ones"])
+    for n in ("wt", "w8", "ft"):
+        fill(T[n][:], 0, [n])
+
+    quant("u", 0, 128, "uv", 0, 512)
+    quant("0", 0, 320, "xt", 0, 1280)
+    V(lambda v: v.tensor_copy(T.qup[:, 0:128].bitcast(dt.uint32), T.qu[:, 0:128].bitcast(dt.uint32).indirect(T.ulist[:, 0:8])), ["qu", "ulist"], ["qup"])
+    V(lambda v: v.tensor_copy(T["sup_p"][:, 0:128], T["su_p"][:, 0:128].indirect(T.ulist[:, 0:8])), ["su_p", "ulist"], ["sup_p"])
+
+    def conts(i, k):
+        lo, hi = 512 * i, 512 * i + 512
+        ts(T.ct[:, 0:2048:4], T.tg[:, lo:hi], cf(11), cf(7), O.is_equal, O.mult, [("tg", lo, hi), K(11), K(7)], ["ct"])
+        quant(k, 0, 512, "ct", 0, 2048)
+    conts(0, "a")
+    ts(T.d0h[:], T.c0[:], cf(21), None, O.add, None, ["c0", K(21)], ["d0h"])
+    V(lambda v: v.tensor_copy(T.c0[:], T.d0h[:]), ["d0h"], ["c0"])
+
+    def unit_tiles():
+        V(lambda v: v.tensor_copy(cf(40), ci(0)), [C(0)], [K(40)])
+        for i in range(2):
+            a, b = 128 * i, 128 * i + 128
+            ts(T.idx[:, a:b], T.ix[:, a:b], cf(40), None, O.is_equal, None, [("ix", a, b), K(40)], [("idx", a, b)])
+        for k, i, val in (("e", 0, 1.0), ("h", 128, 0.5), ("g", 0, 128.0)):
+            for b in range(4):
+                act(T.et[:, 512 * b + b:512 * b + 512:4], T.idx[:, i:i + 128], AF.Copy, [("idx", i, i + 128)], [("et", 512 * b, 512 * b + 512)], scale=val)
+            quant(k, 0, 512, "et", 0, 2048)
+
+    def scan(out, d0, d1, reads, writes):
+        V(lambda v: v.tensor_tensor_scan(out, d0, d1, -4.0, O.max, O.add), reads, writes)
+
+    def stage(st, todo):
+        d0 = "c0"
+        if st:
+            o = ("off12", 16 * st - 16, 16 * st)
+            d0 = "d0h"
+            tt(T.d0h[:], T.wt[:, 0:16].indirect(T.off12[:, o[1]:o[1] + 10]), T.c0[:], O.add, ["wt", o, "c0"], ["d0h"])
+            between(todo)
+        dn, an = "dst%d" % st, "ast%d" % st
+        for h in range(4):
+            a, b = 40 * h, 40 * h + 40
+            scan(T.tt[:, a:b], T[d0][:, a:b], T[dn][:, a:b], [(d0, a, b), dn], [("tt", a, b)])
+        between(todo)
+        tt(T.vv[:], T.tt[:], T[an][:], O.max, ["tt", an], ["vv"])
+        between(todo)
+        V(lambda v: v.tensor_reduce(T.mcol[:, 0:1], T.vv[:], AxisListType.X, O.min), ["vv"], ["mcol"])
+        between(todo)
+        ts(T.mb[:], T.ones[:], T.mcol[:, 0:1], None, O.mult, None, ["ones", "mcol"], ["mb"])
+        between(todo)
+        V(lambda v: v.transpose(T.tb[:], T.mb[:]), ["mb"], ["tb"])
+        between(todo)
+        tt(T.mi[:, 0:8], T.tb[:, 0:8], T.tb[:, 16:24], O.min, ["tb"], ["mi"])
+        between(todo)
+        if st < 2:
+            ts(T.wt[:, 0:8], T.mi[:, 0:8], 0xFFE00, None, O.bitwise_and, None, ["mi"], [("wt", 0, 8)])
+        else:
+            ts(T.w8[:, 0:8], T.mi[:, 0:8], 0xFFE00, 6, O.bitwise_and, O.arith_shift_right, ["mi"], [("w8", 0, 8)])
+        while todo:
+            between(todo)
+
+    def lists(src, dst, at, j, n, mk):
+        k = n // 2
+        return [lambda e=e: ts(T[dst][:, at + e:at + n:2], T[src][:, j + e:16 * n:32], cf(mk), cf(mk + 1), O.mult, O.add, [src, K(mk), K(mk + 1)], [(dst, at + k * e, at + k * e + k)]) for e in range(2)]
+
+    def symbols(part):
+        if part == 0:
+            mm(2, 160, "a", 0, "f", 16, True, False)
+            mm(2, 160, "a", 128, "f", 176, False, True)
+            for i, (a, sh) in enumerate(((256, 0), (256, 144), (384, 16), (384, 160))):
+                mm(3, 160, "a", a, "f", 16 + sh, i == 0, i == 3)
+            sts = ((0, 2),)
+        else:
+            for st in (1, 2):
+                mm(3 + st, 160, "b", 256 * (st - 1), "f", 16, True, False)
+                mm(3 + st, 160, "b", 256 * (st - 1) + 128, "f", 176, False, True)
+            for i, (a, sh) in enumerate(((128, 0), (256, -16), (384, 16))):
+                mm(7, 320, "c", a, "f", 16 + sh, i == 0, i == 2)
+            mm(6, 320, "c", 0, "f", 16)
+            sts = ((1, 4), (2, 5))
+        for st, bank in sts:
+            pb = "pb%d" % bank
+            act(T["dst%d" % st][:], T[pb][:, 0:160], AF.Identity, [pb], ["dst%d" % st], scale=512.0, bias=513.0)
+            act(T["ast%d" % st][:], T[pb][:, 0:160], AF.Abs, [pb, K(20)], ["ast%d" % st], scale=BIG, bias=cf(20))
+        if part:
+            act(T.dow[:], T.pb6[:, 0:320], AF.Identity, ["pb6"], ["dow"], scale=8.0, bias=8.0)
+
+    def decode(r):
+        for i in range(8):
+            k, dst, b = ("e", "fp", i) if i < 4 else ("h", "f2", i - 4)
+            bank = i % 2
+            mm(bank, 320, k, 128 * b, str(r), 0)
+            act(T[dst][:, 320 * b:320 * b + 320], T["pb%d" % bank][:, 0:320], AF.Copy, ["pb%d" % bank], [(dst, 320 * b, 320 * b + 320)])
+
+    def first_table(r):
+        ca, cb = (1.0, 40.0) if r == 0 else (8.0, 1.0)
+
+        def X(i):
+            return T.fx[:, 16 * i:16 * i + 8]
+
+        def F(i):
+            return ("fx", 16 * i, 16 * i + 8)
+        m = T.mi[:, 0:8]
+        return [lambda: ts(X(0), m, 63, None, O.bitwise_and, None, ["mi"], [F(0)]),
+                lambda: ts(X(1), m, 448, 6, O.bitwise_and, O.arith_shift_right, ["mi"], [F(1)]),
+                lambda: ts(X(2), X(0), ca, 1.0, O.mult, O.add, [F(0)], [F(2)]),
+                lambda: ts(X(5), X(1), cb, None, O.mult, None, [F(1)], [F(5)]),
+                lambda: ts(X(4), m, BIG, 512.0, O.is_lt, O.mult, ["mi"], [F(4)]),
+                lambda: tt(X(3), X(2), X(5), O.add, [F(2), F(5)], [F(3)]),
+                lambda: tt(T.ft[:, 0:8], X(3), X(4), O.mult, [F(3), F(4)], [("ft", 0, 8)])]
+
+    def order(r):
+        todo = first_table(r)
+        tt(T.d0o[:], T.w8[:, 0:16].indirect(T.offd[:, 0:20]), T.hrow[:], O.add, ["w8", "offd", "hrow"], ["d0o"])
+        between(todo)
+        between(todo)
+        for h in range(8):
+            a, b = 40 * h, 40 * h + 40
+            scan(T.kap[:, 16 + a:16 + b], T.d0o[:, a:b], T.dow[:, a:b], ["d0o", "dow"], [("kap", 16 + a, 16 + b)])
+        between(todo)
+        V(lambda v: v.transpose(T.kt[:, 0:320], T.kap[:, 16:336]), [("kap", 16, 336)], [("kt", 0, 320)])
+        V(lambda v: v.transpose(T.kt[:, 320:672], T.kap[:]), ["kap"], [("kt", 320, 672)])
+        between(todo)
+        ts(T.ex[:, 0:21], T.kt[:, 0:672:32], cf(23), None, O.mult, None, ["kt", K(23)], [("ex", 0, 21)])
+        ts(T.ex[:, 24:45], T.kt[:, 16:672:32], cf(24), None, O.mult, None, ["kt", K(24)], [("ex", 24, 45)])
+        between(todo)
+        tt(T.my[:, 0:10], T.ex[:, 0:10], T.ex[:, 34:44], O.add, ["ex"], [("my", 0, 10)])
+        tt(T.my[:, 10:20], T.ex[:, 11:21], T.ex[:, 24:34], O.add, ["ex"], [("my", 10, 20)])
+        for q in range(NS):
+            a = 320 * (q % 2)
+            act(T.sj[:, a:a + 320], T.kap[:, 16:336], AF.Sign, [("kap", 16, 336), ("my", q, q + 1)], [("sj", a, a + 320), ("acc", q, q + 1)], scale=-1.0, bias=T.my[:, q:q + 1], accum_out=T.acc[:, q:q + 1])
+        V(lambda v: v.tensor_copy(T.ku[:], T.kap[:, 16:336]), [("kap", 16, 336)], ["ku"])
+        between(todo)
+
+        def less(p):
+            a = 320 * (p % 3)
+            ts(T.fab[:, a:a + 320], T.ku[:], T.my[:, NS + p:NS + p + 1], None, O.is_lt, None, ["ku", ("my", NS + p, NS + p + 1)], [("fab", a, a + 320)])
+        less(0)
+        for p in range(NV):
+            if p + 1 < NV:
+                less(p + 1)
+            a, lo = 320 * (p % 3), 160 * p
+            V(lambda v: v.tensor_tensor_scan(T.scn[:, lo:lo + 160], T.fab[:, a:a + 160], T.fab[:, a + 160:a + 320], -160.0, O.add, O.add), [("fab", a, a + 320)], [("scn", lo, lo + 160)])
+            between(todo)
+        si = "si0" if r == 0 else "si1"
+        tt(T.vrow[:], T.ft[:, 0:16].indirect(T.offd[:, 0:20]), T[si][:], O.add, ["ft", "offd", si], ["vrow"])
+        ts(T.rx[:, NS:20], T.scn[:, 159:160 * NV:160], 160.0, None, O.add, None, ["scn"], [("rx", NS, 20)])
+        ts(T.rx[:, 0:NS], T.acc[:, 0:NS], 0.5, 159.5, O.mult, O.add, ["acc"], [("rx", 0, NS)])
+        ts(T.rx[:, 32:52], T.rx[:, 0:20], 496, None, O.bitwise_and, None, [("rx", 0, 20)], [("rx", 32, 52)])
+        tt(T.rx[:, 64:84], T.rx[:, 0:20], T.rx[:, 32:52], O.add, [("rx", 0, 52)], [("rx", 64, 84)])
+        for e in range(2):
+            ts(T.offs[:, e:20:2], T.rx[:, 64 + 10 * e:74 + 10 * e], cf(22), None, O.add, None, [("rx", 64, 84), K(22)], [("offs", 10 * e, 10 * e + 10)])
+        V(lambda v: v.tensor_copy(T.win[:, 0:640].indirect(T.offs[:, 0:20]), T.vrow[:]), ["vrow", "offs"], ["win"])
+
+    def L(i):
+        return T.lx[:, 16 * i:16 * i + 10]
+
+    def LR(i):
+        return ("lx", 16 * i, 16 * i + 10)
+
+    def plane(n, b):
+        return (n, 320 * b, 320 * b + 320)
+
+    def laid(r):
+        V(lambda v: v.transpose(T.tw[:, 0:320], T.win[:, 0:320]), [("win", 0, 320)], [("tw", 0, 320)])
+        tt(L(0), T.tw[:, 0:320:32], T.tw[:, 16:320:32], O.add, [("tw", 0, 320)], [LR(0)])
+        ts(L(1), L(0), 511, None, O.bitwise_and, None, [LR(0)], [LR(1)])
+        ts(L(2), L(0), 9, None, O.arith_shift_right, None, [LR(0)], [LR(2)])
+        ts(T.ll[:, 0:10], L(1), -1.0, None, O.add, None, [LR(1)], ["ll"])
+        for b in range(4):
+            act(T.pz[:, 160 * b:160 * b + 160], T.fp[:, 320 * b:320 * b + 320].indirect(T.ll[:, 0:10]), AF.Copy, [plane("fp", b), "ll"], [("pz", 160 * b, 160 * b + 160)], scale=0.5)
+        ts(L(3), L(2), 0.0, None, O.is_equal, None, [LR(2)], [LR(3)])
+        tt(L(4), L(3), L(1), O.mult, [LR(3), LR(1)], [LR(4)])
+        tt(L(5), L(4), L(2), O.add, [LR(4), LR(2)], [LR(5)])
+        ts(T.bl[:, 0:10], L(5), -1.0, None, O.add, None, [LR(5)], ["bl"])
+        for b in range(4):
+            tt(T.zt[:, b:640:4], T.f2[:, 320 * b:320 * b + 320].indirect(T.bl[:, 0:10]), T.pz[:, 160 * b:160 * b + 160], O.add,
+               [plane("f2", b), "bl", ("pz", 160 * b, 160 * b + 160)], [("zt", 160 * b, 160 * b + 160)])
+        z, l = "z%d" % r, "l%d" % r
+        quant(z, 0, 160, "zt", 0, 640)
+        rid, pid, _ = topo.addr(nxt)
+        m = topo.mask(core, nxt)
+        arr = "arr%d" % r
+        waits("G", accesses(["q" + z, "s" + z + "_p"], []))
+        g.remote_dma(T["q" + l][:, 0:160].bitcast(dt.uint8), T["q" + z][:, 0:160].bitcast(dt.uint8), T.sem[arr], T.sem["loc"], pid, rid, m)
+        g.remote_dma(T["s" + l + "_p"][:, 0:160], T["s" + z + "_p"][:, 0:160], T.sem[arr], T.sem["loc"], pid, rid, m)
+        k = 2 * len(topo.engines(core, nxt))
+        count["loc"] = count.get("loc", 0) + k
+        count[arr] = k
+        for n in ("q" + l, "s" + l + "_p"):
+            hist[n] = [[0, 160, "w", arr, k]]
+
+    def kept(r):
+        V(lambda v: v.transpose(T.tw[:, 320:640], T.win[:, 320:640]), [("win", 320, 640)], [("tw", 320, 640)])
+        tt(L(6), T.tw[:, 320:640:32], T.tw[:, 336:640:32], O.add, [("tw", 320, 640)], [LR(6)])
+        ts(L(7), L(6), 511, None, O.bitwise_and, None, [LR(6)], [LR(7)])
+        ts(T.kl[:, 0:10], L(7), -1.0, None, O.add, None, [LR(7)], ["kl"])
+        for b in range(4):
+            rd, wr = [plane("fp", b), "kl"], [("xk", 160 * b, 160 * b + 160)]
+            if b % 2:
+                act(T.xk[:, b:640:4], T.fp[:, 320 * b:320 * b + 320].indirect(T.kl[:, 0:10]), AF.Copy, rd, wr)
+            else:
+                V(lambda v: v.tensor_copy(T.xk[:, b:640:4], T.fp[:, 320 * b:320 * b + 320].indirect(T.kl[:, 0:10])), rd, wr)
+        quant(str(r + 1), 0, 160, "xk", 0, 640)
+
+    def arrive(r):
+        for b in range(4):
+            mm(2 + b, 160, "w", 128 * b, "l%d" % r, 0, True, False)
+            mm(2 + b, 160, "g", 128 * b, "l%d" % r, 0, False, True)
+        for b in range(4):
+            pb, wr = "pb%d" % (2 + b), [("xh", 160 * b, 160 * b + 160)]
+            if b % 2:
+                ts(T.xh[:, b:640:4], T[pb][:, 0:160], 0.0078125, None, O.mult, None, [pb], wr)
+            else:
+                act(T.xh[:, b:640:4], T[pb][:, 0:160], AF.Copy, [pb], wr, scale=0.0078125)
+        quant(str(r + 1), 160, 320, "xh", 0, 640)
+
+    def flags(half, bank):
+        for h in range(8):
+            a = 40 * h + 20 * half
+            tt(T.fl[:, 64 + 4 * a:144 + 4 * a:4], T["pb%d" % bank][:, h:160:8], T.th[:, a:a + 20], O.is_gt, ["pb%d" % bank, "th"], [("fl", 64 + 4 * a, 144 + 4 * a)])
+
+    for r in range(3):
+        if r == 0:
+            mm(0, 320, "up", 0, "0", 0)
+            tt(T.fl[:, 64:1344:4], T.pb0[:, 0:320], T.th[:], O.is_gt, ["pb0", "th"], ["fl"])
+        else:
+            mm(1, 160, "up", 0, str(r), 160)
+            flags(1, 1)
+        quant("f", 0, 352, "fl", 0, 1408)
+        symbols(0)
+        if r == 0:
+            conts(1, "b")
+            conts(2, "c")
+            fill(T.kap[:], 0.0, ["kap"])
+            fill(T.win[:], 0.0, ["win"])
+        symbols(1)
+        if r == 0:
+            unit_tiles()
+        decode(r)
+        half = [lambda: V(lambda v: v.transpose(T.tl[:], T.pb3[:, 0:160]), ["pb3"], ["tl"])] + lists("tl", "off12", 0, 0, 10, 25) + lists("tl", "off12", 16, 2, 10, 27)
+        full = [lambda: V(lambda v: v.transpose(T.tlo[:], T.pb7[:, 0:320]), ["pb7"], ["tlo"])] + lists("tlo", "offd", 0, 0, 20, 29)
+        stage(0, half)
+        stage(1, [])
+        stage(2, full)
+        order(r)
+        laid(r)
+        kept(r)
+        if r < 2:
+            mm(0, 160, "up", 0, str(r + 1), 0)
+            flags(0, 0)
+        else:
+            for e in range(2):
+                V(lambda v: v.tensor_copy(T.offo[:, e:20:2], T.rx[:, 10 * e:10 * e + 10]), [("rx", 0, 20)], [("offo", 10 * e, 10 * e + 10)])
+            V(lambda v: v.tensor_copy(T.oprow[:, 0:320].indirect(T.offo[:, 0:20]), T.ccol[:]), ["ccol", "offo"], ["oprow"])
+            for k in range(8):
+                dma("Y", T.op[k:k + 1, :], T.oprow[16 * k:16 * k + 1, :], ["oprow"], [], "doy")
+
+            def N(i):
+                return T.nx[:, 20 * i:20 * i + 20]
+
+            def NR(i):
+                return ("nx", 20 * i, 20 * i + 20)
+            V(lambda v: v.tensor_copy(cf(41), ci(RK)), [C(RK)], [K(41)])
+            ts(N(1), N(0), cf(41), None, O.add, None, [NR(0), K(41)], [NR(1)])
+            ts(N(0), N(1), 205.0, None, O.mult, None, [NR(1)], [NR(0)])
+            ts(N(2), N(0), 13, None, O.arith_shift_right, None, [NR(0)], [NR(2)])
+            ts(N(0), N(2), -319.0, None, O.mult, None, [NR(2)], [NR(0)])
+            ts(N(2), N(1), 8.0, None, O.mult, None, [NR(1)], [NR(2)])
+            tt(T.fx[:, 96:116], N(0), N(2), O.add, [NR(0), NR(2)], [("fx", 96, 116)])
+            V(lambda v: v.tensor_copy(T.nat[:, 0:20], T.fx[:, 96:116]), [("fx", 96, 116)], ["nat"])
+            quant("v", 0, 128, "uv", 512, 1024)
+        arrive(r)
+    V(lambda v: v.tensor_copy(T.qn[:, 0:320].bitcast(dt.uint32), T.q3[:, 0:320].bitcast(dt.uint32).indirect(T.nat[:, 0:20])), ["q3", "nat"], ["qn"])
+    act(T["sn_p"][:, 0:320], T["s3_p"][:, 0:320].indirect(T.nat[:, 0:20]), AF.Copy, ["s3_p", "nat"], ["sn_p"])
+    mm(0, 320, "v", 0, "n", 0)
+    dma("Y", T.oc[:], T.qn[:].bitcast(dt.uint8), ["qn"], [], "doy")
+    for k in range(4):
+        dma("S" if k % 2 else "Y", T.osc[4 * k:4 * k + 4, :], T["sn_p"][32 * k:32 * k + 4, :], ["sn_p"], [], "doa" if k % 2 else "doy")
+    V(lambda v: v.tensor_copy(T.yo[:], T.pb0[:, 0:320]), ["pb0"], ["yo"])
+    dma("S", T.y[:], T.yo[:], ["yo"], [], "doa")
+    for s in sorted(count):
+        if known["G"].get(s, 0) < count[s]:
+            g.wait_ge(T.sem[s], count[s])

@@ -1,6 +1,6 @@
 from concourse.mybir import dt, AluOpType as O, AxisListType, ActivationFunctionType as AF
 
-NS = 11
+NS = 10
 NV = 20 - NS
 HUGE = 1.0e25
 BIG = float(2 ** 20)
@@ -21,7 +21,8 @@ def _decl():
     sb("fl", 1408, "bfloat16")
     sb("fab", 960, "bfloat16")
     sb("scn", 160 * NV, "bfloat16")
-    sb("idx", 256, "bfloat16")
+    sb("idx ix", 256, "bfloat16")
+    sb("tg", 1536, "bfloat16")
     for k, n in (("u", 128), ("up", 128), ("v", 128), ("w", 512), ("e", 512), ("h", 512), ("g", 512), ("a", 512), ("b", 512), ("c", 512), ("f", 352), ("n", 320)):
         d["q" + k] = ("sbuf", [128, n], F4)
         d["s" + k + "_p"] = ("sbuf", [128, n], "uint8")
@@ -32,20 +33,19 @@ def _decl():
         for k in ("z", "l"):
             d["q%s%d" % (k, r)] = ("sbuf", [128, 160], F4)
             d["s%s%d_p" % (k, r)] = ("sbuf", [128, 160], "uint8")
-    sb("tg", 1536, "float32")
     sb("par th hrow si0 si1 ccol d0o dow vrow yo oprow tlo", 320, "float32")
     sb("c0 d0h tt vv dst0 dst1 dst2 ast0 ast1 ast2 tl", 160, "float32")
-    sb("ix", 256, "float32")
     sb("kap", 352, "float32")
     sb("kt", 672, "float32")
     sb("ex", 48, "float32")
     sb("my acc", 20, "float32")
     sb("win tw", 640, "float32")
     sb("mcol", 8, "float32")
-    sb("ones mb tb", 32, "float32")
-    sb("cf", 64, "float32")
+    sb("top mb tb", 32, "float32")
+    sb("cf rf", 64, "float32")
     sb("ci mi wt w8 ft ub", 16, "int32")
-    sb("fx lx rx", 128, "int32")
+    sb("fx lx", 128, "int32")
+    sb("rx", 32, "int32")
     sb("nx", 64, "int32")
     sb("off12 offd offs offo nat", 32, "uint16")
     sb("ll bl kl ulist", 16, "uint16")
@@ -171,12 +171,12 @@ def rank_program(g, core, T, topo):
     fill(T.tg[:, 256:512], -1.0, [("tg", 256, 512)])
     iota(T.ci[:, 0:1], [[1, 1]], 0, 1, [("ci", 0, 1)], f=False)
     iota(T.ub[:, 0:8], [[16, 8]], 0, 0, ["ub"], f=False)
-    iota(T.par[:], [[0, 10], [1, 2], [0, 16]], 0, 0, ["par"])
     iota(T.tg[:, 0:128], [[0, 4], [100, 2], [0, 16]], 0, 0, [("tg", 0, 128)])
     iota(T.tg[:, 128:256], [[0, 4], [100, 2], [0, 16]], -100, 0, [("tg", 128, 256)])
     for base, jj, code in ((256, 0, 8), (384, 1, 16)):
         iota(T.tg[:, base + jj:base + 128:32], [[1, 2], [0, 2]], code, 0, [("tg", base, base + 64)])
         iota(T.tg[:, base + jj + 2:base + 128:32], [[1, 4]], code, 0, [("tg", base + 64, base + 128)])
+    iota(T.par[:], [[0, 10], [1, 2], [0, 16]], 0, 0, ["par"])
     iota(T.c0[:], [[64, 4], [1, 40]], -1, 0, ["c0"])
     for h in range(2):
         for k in range(2):
@@ -237,40 +237,47 @@ def rank_program(g, core, T, topo):
     act(T.th[:], T.par[:], AF.Identity, ["par", K(14), K(13)], ["th"], scale=cf(14), bias=cf(13))
     for b in range(4):
         act(T.et[:, 512 * b:512 * b + 512], T.zz[:], AF.Copy, ["zz"], [("et", 512 * b, 512 * b + 512)])
-    ts(cf(20), ci(SG), -BIG, None, O.mult, None, [C(SG)], [K(20)])
-    ts(cf(21), ci(HF), 256.0, None, O.mult, None, [C(HF)], [K(21)])
-    ts(cf(22), ci(HF), 16.0, None, O.mult, None, [C(HF)], [K(22)])
-    ts(cf(23), ci(HF), 0.0, None, O.is_equal, None, [C(HF)], [K(23)])
-    ts(cf(24), ci(HF), 1.0, None, O.is_equal, None, [C(HF)], [K(24)])
-    for i, (src, least) in enumerate(((BK, 2.0), (BK, 1.0), (GR, 1.0))):
-        ts(cf(25 + 2 * i), ci(src), least, None, O.is_ge, None, [C(src)], [K(25 + 2 * i)])
-        ts(cf(26 + 2 * i), ci(src), least, 8.0, O.is_lt, O.mult, [C(src)], [K(26 + 2 * i)])
-    fill(T.ones[:], 1.0, ["ones"])
-    for n in ("wt", "w8", "ft"):
-        fill(T[n][:], 0, [n])
-
-    quant("u", 0, 128, "uv", 0, 512)
-    quant("0", 0, 320, "xt", 0, 1280)
-    V(lambda v: v.tensor_copy(T.qup[:, 0:128].bitcast(dt.uint32), T.qu[:, 0:128].bitcast(dt.uint32).indirect(T.ulist[:, 0:8])), ["qu", "ulist"], ["qup"])
-    V(lambda v: v.tensor_copy(T["sup_p"][:, 0:128], T["su_p"][:, 0:128].indirect(T.ulist[:, 0:8])), ["su_p", "ulist"], ["sup_p"])
 
     def conts(i, k):
         lo, hi = 512 * i, 512 * i + 512
         ts(T.ct[:, 0:2048:4], T.tg[:, lo:hi], cf(11), cf(7), O.is_equal, O.mult, [("tg", lo, hi), K(11), K(7)], ["ct"])
         quant(k, 0, 512, "ct", 0, 2048)
     conts(0, "a")
+    quant("u", 0, 128, "uv", 0, 512)
+    quant("0", 0, 320, "xt", 0, 1280)
+    V(lambda v: v.tensor_copy(T.qup[:, 0:128].bitcast(dt.uint32), T.qu[:, 0:128].bitcast(dt.uint32).indirect(T.ulist[:, 0:8])), ["qu", "ulist"], ["qup"])
+    V(lambda v: v.tensor_copy(T["sup_p"][:, 0:128], T["su_p"][:, 0:128].indirect(T.ulist[:, 0:8])), ["su_p", "ulist"], ["sup_p"])
+    ts(cf(20), ci(SG), -BIG, None, O.mult, None, [C(SG)], [K(20)])
+    ts(cf(21), ci(HF), 256.0, None, O.mult, None, [C(HF)], [K(21)])
+    ts(cf(22), ci(HF), 16.0, None, O.mult, None, [C(HF)], [K(22)])
     ts(T.d0h[:], T.c0[:], cf(21), None, O.add, None, ["c0", K(21)], ["d0h"])
+    ts(cf(23), ci(HF), 0.0, None, O.is_equal, None, [C(HF)], [K(23)])
+    ts(cf(24), ci(HF), 1.0, None, O.is_equal, None, [C(HF)], [K(24)])
     V(lambda v: v.tensor_copy(T.c0[:], T.d0h[:]), ["d0h"], ["c0"])
+    for i, (src, least) in enumerate(((BK, 2.0), (BK, 1.0), (GR, 1.0))):
+        ts(cf(25 + 2 * i), ci(src), least, None, O.is_ge, None, [C(src)], [K(25 + 2 * i)])
+        ts(cf(26 + 2 * i), ci(src), least, 8.0, O.is_lt, O.mult, [C(src)], [K(26 + 2 * i)])
+    fill(T.top[:], 3.0e7, ["top"])
+    for n in ("wt", "w8", "ft"):
+        fill(T[n][:], 0, [n])
+    UNITS = (("e", 0, 1.0), ("h", 128, 0.5), ("g", 0, 128.0))
 
-    def unit_tiles():
+    def unit(j):
+        k, i, val = UNITS[j]
+        for b in range(4):
+            act(T.et[:, 512 * b + b:512 * b + 512:4], T.idx[:, i:i + 128], AF.Copy, [("idx", i, i + 128)], [("et", 512 * b, 512 * b + 512)], scale=val)
+
+    def unit_done(j):
+        quant(UNITS[j][0], 0, 512, "et", 0, 2048)
+        if j < 2:
+            unit(j + 1)
+
+    def units():
         V(lambda v: v.tensor_copy(cf(40), ci(0)), [C(0)], [K(40)])
         for i in range(2):
             a, b = 128 * i, 128 * i + 128
             ts(T.idx[:, a:b], T.ix[:, a:b], cf(40), None, O.is_equal, None, [("ix", a, b), K(40)], [("idx", a, b)])
-        for k, i, val in (("e", 0, 1.0), ("h", 128, 0.5), ("g", 0, 128.0)):
-            for b in range(4):
-                act(T.et[:, 512 * b + b:512 * b + 512:4], T.idx[:, i:i + 128], AF.Copy, [("idx", i, i + 128)], [("et", 512 * b, 512 * b + 512)], scale=val)
-            quant(k, 0, 512, "et", 0, 2048)
+        unit(0)
 
     def scan(out, d0, d1, reads, writes):
         V(lambda v: v.tensor_tensor_scan(out, d0, d1, -4.0, O.max, O.add), reads, writes)
@@ -278,20 +285,20 @@ def rank_program(g, core, T, topo):
     def stage(st, todo):
         d0 = "c0"
         if st:
-            o = ("off12", 16 * st - 16, 16 * st)
+            o = 16 * st - 16
             d0 = "d0h"
-            tt(T.d0h[:], T.wt[:, 0:16].indirect(T.off12[:, o[1]:o[1] + 10]), T.c0[:], O.add, ["wt", o, "c0"], ["d0h"])
-            between(todo)
+            for a, b in ((0, 96), (96, 160)):
+                tt(T.d0h[:, a:b], T.wt[:, 0:16].indirect(T.off12[:, o + a // 16:o + b // 16]), T.c0[:, a:b], O.add, ["wt", ("off12", o, o + 16), "c0"], [("d0h", a, b)])
         dn, an = "dst%d" % st, "ast%d" % st
         for h in range(4):
             a, b = 40 * h, 40 * h + 40
             scan(T.tt[:, a:b], T[d0][:, a:b], T[dn][:, a:b], [(d0, a, b), dn], [("tt", a, b)])
+        for a, b in ((0, 80), (80, 160)):
+            tt(T.vv[:, a:b], T.tt[:, a:b], T[an][:, a:b], O.max, [("tt", a, b), an], [("vv", a, b)])
+        for i in range(2):
+            V(lambda v: v.tensor_reduce(T.mcol[:, i:i + 1], T.vv[:, 80 * i:80 * i + 80], AxisListType.X, O.min), [("vv", 80 * i, 80 * i + 80)], [("mcol", i, i + 1)])
         between(todo)
-        tt(T.vv[:], T.tt[:], T[an][:], O.max, ["tt", an], ["vv"])
-        between(todo)
-        V(lambda v: v.tensor_reduce(T.mcol[:, 0:1], T.vv[:], AxisListType.X, O.min), ["vv"], ["mcol"])
-        between(todo)
-        ts(T.mb[:], T.ones[:], T.mcol[:, 0:1], None, O.mult, None, ["ones", "mcol"], ["mb"])
+        ts(T.mb[:], T.top[:], T.mcol[:, 0:1], T.mcol[:, 1:2], O.min, O.min, ["top", "mcol"], ["mb"])
         between(todo)
         V(lambda v: v.transpose(T.tb[:], T.mb[:]), ["mb"], ["tb"])
         between(todo)
@@ -309,25 +316,27 @@ def rank_program(g, core, T, topo):
         return [lambda e=e: ts(T[dst][:, at + e:at + n:2], T[src][:, j + e:16 * n:32], cf(mk), cf(mk + 1), O.mult, O.add, [src, K(mk), K(mk + 1)], [(dst, at + k * e, at + k * e + k)]) for e in range(2)]
 
     def symbols(part):
+        sts = ()
         if part == 0:
             mm(2, 160, "a", 0, "f", 16, True, False)
             mm(2, 160, "a", 128, "f", 176, False, True)
             for i, (a, sh) in enumerate(((256, 0), (256, 144), (384, 16), (384, 160))):
                 mm(3, 160, "a", a, "f", 16 + sh, i == 0, i == 3)
             sts = ((0, 2),)
-        else:
+        elif part == 1:
             for st in (1, 2):
                 mm(3 + st, 160, "b", 256 * (st - 1), "f", 16, True, False)
                 mm(3 + st, 160, "b", 256 * (st - 1) + 128, "f", 176, False, True)
+            sts = ((1, 4), (2, 5))
+        else:
             for i, (a, sh) in enumerate(((128, 0), (256, -16), (384, 16))):
                 mm(7, 320, "c", a, "f", 16 + sh, i == 0, i == 2)
             mm(6, 320, "c", 0, "f", 16)
-            sts = ((1, 4), (2, 5))
         for st, bank in sts:
             pb = "pb%d" % bank
             act(T["dst%d" % st][:], T[pb][:, 0:160], AF.Identity, [pb], ["dst%d" % st], scale=512.0, bias=513.0)
             act(T["ast%d" % st][:], T[pb][:, 0:160], AF.Abs, [pb, K(20)], ["ast%d" % st], scale=BIG, bias=cf(20))
-        if part:
+        if part == 2:
             act(T.dow[:], T.pb6[:, 0:320], AF.Identity, ["pb6"], ["dow"], scale=8.0, bias=8.0)
 
     def decode(r):
@@ -356,15 +365,15 @@ def rank_program(g, core, T, topo):
 
     def order(r):
         todo = first_table(r)
-        tt(T.d0o[:], T.w8[:, 0:16].indirect(T.offd[:, 0:20]), T.hrow[:], O.add, ["w8", "offd", "hrow"], ["d0o"])
-        between(todo)
-        between(todo)
+        for a in (0, 160):
+            tt(T.d0o[:, a:a + 160], T.w8[:, 0:16].indirect(T.offd[:, a // 16:a // 16 + 10]), T.hrow[:, a:a + 160], O.add, ["w8", "offd", "hrow"], [("d0o", a, a + 160)])
         for h in range(8):
             a, b = 40 * h, 40 * h + 40
-            scan(T.kap[:, 16 + a:16 + b], T.d0o[:, a:b], T.dow[:, a:b], ["d0o", "dow"], [("kap", 16 + a, 16 + b)])
-        between(todo)
-        V(lambda v: v.transpose(T.kt[:, 0:320], T.kap[:, 16:336]), [("kap", 16, 336)], [("kt", 0, 320)])
+            scan(T.kap[:, 16 + a:16 + b], T.d0o[:, a:b], T.dow[:, a:b], [("d0o", a, b), "dow"], [("kap", 16 + a, 16 + b)])
+        for a in (0, 160):
+            V(lambda v: v.transpose(T.kt[:, a:a + 160], T.kap[:, 16 + a:176 + a]), [("kap", 16 + a, 176 + a)], [("kt", a, a + 160)])
         V(lambda v: v.transpose(T.kt[:, 320:672], T.kap[:]), ["kap"], [("kt", 320, 672)])
+        between(todo)
         between(todo)
         ts(T.ex[:, 0:21], T.kt[:, 0:672:32], cf(23), None, O.mult, None, ["kt", K(23)], [("ex", 0, 21)])
         ts(T.ex[:, 24:45], T.kt[:, 16:672:32], cf(24), None, O.mult, None, ["kt", K(24)], [("ex", 24, 45)])
@@ -389,12 +398,12 @@ def rank_program(g, core, T, topo):
             between(todo)
         si = "si0" if r == 0 else "si1"
         tt(T.vrow[:], T.ft[:, 0:16].indirect(T.offd[:, 0:20]), T[si][:], O.add, ["ft", "offd", si], ["vrow"])
-        ts(T.rx[:, NS:20], T.scn[:, 159:160 * NV:160], 160.0, None, O.add, None, ["scn"], [("rx", NS, 20)])
-        ts(T.rx[:, 0:NS], T.acc[:, 0:NS], 0.5, 159.5, O.mult, O.add, ["acc"], [("rx", 0, NS)])
-        ts(T.rx[:, 32:52], T.rx[:, 0:20], 496, None, O.bitwise_and, None, [("rx", 0, 20)], [("rx", 32, 52)])
-        tt(T.rx[:, 64:84], T.rx[:, 0:20], T.rx[:, 32:52], O.add, [("rx", 0, 52)], [("rx", 64, 84)])
+        for src, n, a, b, m, c in (("scn", slice(159, 160 * NV, 160), NS, 20, 0.0625, 10.0), ("acc", slice(0, NS), 0, NS, 0.03125, 9.96875)):
+            ts(T.rf[:, a:b], T[src][:, n], m, c, O.mult, O.add, [src], [("rf", a, b)])
+            ts(T.rx[:, a:b], T[src][:, n], m, c - 0.46875, O.mult, O.add, [src], [("rx", a, b)])
+        tt(T.rf[:, 32:52], T.rf[:, 0:20], T.rx[:, 0:20], O.add, [("rf", 0, 20), ("rx", 0, 20)], [("rf", 32, 52)])
         for e in range(2):
-            ts(T.offs[:, e:20:2], T.rx[:, 64 + 10 * e:74 + 10 * e], cf(22), None, O.add, None, [("rx", 64, 84), K(22)], [("offs", 10 * e, 10 * e + 10)])
+            ts(T.offs[:, e:20:2], T.rf[:, 32 + 10 * e:42 + 10 * e], 16.0, cf(22), O.mult, O.add, [("rf", 32, 52), K(22)], [("offs", 10 * e, 10 * e + 10)])
         V(lambda v: v.tensor_copy(T.win[:, 0:640].indirect(T.offs[:, 0:20]), T.vrow[:]), ["vrow", "offs"], ["win"])
 
     def L(i):
@@ -410,11 +419,11 @@ def rank_program(g, core, T, topo):
         V(lambda v: v.transpose(T.tw[:, 0:320], T.win[:, 0:320]), [("win", 0, 320)], [("tw", 0, 320)])
         tt(L(0), T.tw[:, 0:320:32], T.tw[:, 16:320:32], O.add, [("tw", 0, 320)], [LR(0)])
         ts(L(1), L(0), 511, None, O.bitwise_and, None, [LR(0)], [LR(1)])
+        ts(L(3), L(0), 512.0, None, O.is_lt, None, [LR(0)], [LR(3)])
         ts(L(2), L(0), 9, None, O.arith_shift_right, None, [LR(0)], [LR(2)])
         ts(T.ll[:, 0:10], L(1), -1.0, None, O.add, None, [LR(1)], ["ll"])
         for b in range(4):
             act(T.pz[:, 160 * b:160 * b + 160], T.fp[:, 320 * b:320 * b + 320].indirect(T.ll[:, 0:10]), AF.Copy, [plane("fp", b), "ll"], [("pz", 160 * b, 160 * b + 160)], scale=0.5)
-        ts(L(3), L(2), 0.0, None, O.is_equal, None, [LR(2)], [LR(3)])
         tt(L(4), L(3), L(1), O.mult, [LR(3), LR(1)], [LR(4)])
         tt(L(5), L(4), L(2), O.add, [LR(4), LR(2)], [LR(5)])
         ts(T.bl[:, 0:10], L(5), -1.0, None, O.add, None, [LR(5)], ["bl"])
@@ -460,6 +469,12 @@ def rank_program(g, core, T, topo):
                 act(T.xh[:, b:640:4], T[pb][:, 0:160], AF.Copy, [pb], wr, scale=0.0078125)
         quant(str(r + 1), 160, 320, "xh", 0, 640)
 
+    def product_v(half):
+        mm(half, 160, "v", 0, "3", 160 * half)
+        for h in range(8):
+            a = 40 * h + 20 * half
+            act(T.yo[:, a:a + 20], T["pb%d" % half][:, h:160:8], AF.Copy, ["pb%d" % half], [("yo", a, a + 20)])
+
     def flags(half, bank):
         for h in range(8):
             a = 40 * h + 20 * half
@@ -468,25 +483,30 @@ def rank_program(g, core, T, topo):
     for r in range(3):
         if r == 0:
             mm(0, 320, "up", 0, "0", 0)
-            tt(T.fl[:, 64:1344:4], T.pb0[:, 0:320], T.th[:], O.is_gt, ["pb0", "th"], ["fl"])
+            for a in (0, 160):
+                tt(T.fl[:, 64 + 4 * a:704 + 4 * a:4], T.pb0[:, a:a + 160], T.th[:, a:a + 160], O.is_gt, ["pb0", "th"], [("fl", 64 + 4 * a, 704 + 4 * a)])
         else:
             mm(1, 160, "up", 0, str(r), 160)
             flags(1, 1)
-        quant("f", 0, 352, "fl", 0, 1408)
+        quant("f", 0, 176, "fl", 0, 704)
+        quant("f", 176, 352, "fl", 704, 1408)
         symbols(0)
-        if r == 0:
-            conts(1, "b")
-            conts(2, "c")
-            fill(T.kap[:], 0.0, ["kap"])
-            fill(T.win[:], 0.0, ["win"])
-        symbols(1)
-        if r == 0:
-            unit_tiles()
-        decode(r)
         half = [lambda: V(lambda v: v.transpose(T.tl[:], T.pb3[:, 0:160]), ["pb3"], ["tl"])] + lists("tl", "off12", 0, 0, 10, 25) + lists("tl", "off12", 16, 2, 10, 27)
         full = [lambda: V(lambda v: v.transpose(T.tlo[:], T.pb7[:, 0:320]), ["pb7"], ["tlo"])] + lists("tlo", "offd", 0, 0, 20, 29)
-        stage(0, half)
-        stage(1, [])
+        if r == 0:
+            conts(1, "b")
+            symbols(1)
+            stage(0, half + [lambda: conts(2, "c"), units])
+            symbols(2)
+            stage(1, [lambda: fill(T.kap[:], 0.0, ["kap"]), lambda: unit_done(0), lambda: fill(T.win[:], 0.0, ["win"]), lambda: unit_done(1)])
+            unit_done(2)
+            decode(r)
+        else:
+            symbols(1)
+            symbols(2)
+            decode(r)
+            stage(0, half)
+            stage(1, [])
         stage(2, full)
         order(r)
         laid(r)
@@ -495,8 +515,10 @@ def rank_program(g, core, T, topo):
             mm(0, 160, "up", 0, str(r + 1), 0)
             flags(0, 0)
         else:
+            quant("v", 0, 128, "uv", 512, 1024)
+            product_v(0)
             for e in range(2):
-                V(lambda v: v.tensor_copy(T.offo[:, e:20:2], T.rx[:, 10 * e:10 * e + 10]), [("rx", 0, 20)], [("offo", 10 * e, 10 * e + 10)])
+                ts(T.offo[:, e:20:2], T.rf[:, 10 * e:10 * e + 10], 16.0, None, O.mult, None, [("rf", 0, 20)], [("offo", 10 * e, 10 * e + 10)])
             V(lambda v: v.tensor_copy(T.oprow[:, 0:320].indirect(T.offo[:, 0:20]), T.ccol[:]), ["ccol", "offo"], ["oprow"])
             for k in range(8):
                 dma("Y", T.op[k:k + 1, :], T.oprow[16 * k:16 * k + 1, :], ["oprow"], [], "doy")
@@ -514,16 +536,14 @@ def rank_program(g, core, T, topo):
             ts(N(2), N(1), 8.0, None, O.mult, None, [NR(1)], [NR(2)])
             tt(T.fx[:, 96:116], N(0), N(2), O.add, [NR(0), NR(2)], [("fx", 96, 116)])
             V(lambda v: v.tensor_copy(T.nat[:, 0:20], T.fx[:, 96:116]), [("fx", 96, 116)], ["nat"])
-            quant("v", 0, 128, "uv", 512, 1024)
         arrive(r)
-    V(lambda v: v.tensor_copy(T.qn[:, 0:320].bitcast(dt.uint32), T.q3[:, 0:320].bitcast(dt.uint32).indirect(T.nat[:, 0:20])), ["q3", "nat"], ["qn"])
-    act(T["sn_p"][:, 0:320], T["s3_p"][:, 0:320].indirect(T.nat[:, 0:20]), AF.Copy, ["s3_p", "nat"], ["sn_p"])
-    mm(0, 320, "v", 0, "n", 0)
-    dma("Y", T.oc[:], T.qn[:].bitcast(dt.uint8), ["qn"], [], "doy")
+    product_v(1)
+    dma("S", T.y[:], T.yo[:], ["yo"], [], "doa")
+    V(lambda v: v.tensor_copy(T["sn_p"][:, 0:320], T["s3_p"][:, 0:320].indirect(T.nat[:, 0:20])), ["s3_p", "nat"], ["sn_p"])
     for k in range(4):
         dma("S" if k % 2 else "Y", T.osc[4 * k:4 * k + 4, :], T["sn_p"][32 * k:32 * k + 4, :], ["sn_p"], [], "doa" if k % 2 else "doy")
-    V(lambda v: v.tensor_copy(T.yo[:], T.pb0[:, 0:320]), ["pb0"], ["yo"])
-    dma("S", T.y[:], T.yo[:], ["yo"], [], "doa")
+    V(lambda v: v.tensor_copy(T.qn[:, 0:320].bitcast(dt.uint32), T.q3[:, 0:320].bitcast(dt.uint32).indirect(T.nat[:, 0:20])), ["q3", "nat"], ["qn"])
+    dma("Y", T.oc[:], T.qn[:].bitcast(dt.uint8), ["qn"], [], "doy")
     for s in sorted(count):
         if known["G"].get(s, 0) < count[s]:
             g.wait_ge(T.sem[s], count[s])

from concourse.mybir import dt, AluOpType as O, AxisListType, ActivationFunctionType as AF

NS = 10
NV = 20 - NS
HUGE = 1.0e25
BIG = float(2 ** 20)
F4 = "float8_e4m3fn_x4"


def _decl():
    d = {}

    def sb(names, n, t):
        for k in names.split():
            d[k] = ("sbuf", [128, n], t)
    sb("xt fp f2", 1280, "bfloat16")
    sb("xk xh zt pz sj", 640, "bfloat16")
    sb("uv", 1024, "bfloat16")
    sb("zz", 512, "bfloat16")
    sb("ct et", 2048, "bfloat16")
    sb("fl", 1408, "bfloat16")
    sb("fab", 960, "bfloat16")
    sb("scn", 160 * NV, "bfloat16")
    sb("idx ix", 256, "bfloat16")
    sb("tg", 1536, "bfloat16")
    for k, n in (("u", 128), ("up", 128), ("v", 128), ("w", 512), ("e", 512), ("h", 512), ("g", 512), ("a", 512), ("b", 512), ("c", 512), ("f", 352), ("n", 320)):
        d["q" + k] = ("sbuf", [128, n], F4)
        d["s" + k + "_p"] = ("sbuf", [128, n], "uint8")
    for r in range(4):
        d["q%d" % r] = ("sbuf", [128, 320], F4)
        d["s%d_p" % r] = ("sbuf", [128, 320], "uint8")
    for r in range(3):
        for k in ("z", "l"):
            d["q%s%d" % (k, r)] = ("sbuf", [128, 160], F4)
            d["s%s%d_p" % (k, r)] = ("sbuf", [128, 160], "uint8")
    sb("par th hrow si0 si1 ccol d0o dow vrow yo oprow tlo", 320, "float32")
    sb("c0 d0h tt vv dst0 dst1 dst2 ast0 ast1 ast2 tl", 160, "float32")
    sb("kap", 352, "float32")
    sb("kt", 672, "float32")
    sb("ex", 48, "float32")
    sb("my acc", 20, "float32")
    sb("win tw", 640, "float32")
    sb("mcol", 8, "float32")
    sb("top mb tb", 32, "float32")
    sb("cf rf", 64, "float32")
    sb("ci mi wt w8 ft ub", 16, "int32")
    sb("fx lx", 128, "int32")
    sb("rx", 32, "int32")
    sb("nx", 64, "int32")
    sb("off12 offd offs offo nat", 32, "uint16")
    sb("ll bl kl ulist", 16, "uint16")
    sb("ku", 320, "uint16")
    for b in range(8):
        d["pb%d" % b] = ("psum", [128, 512], "float32")
    return d


SCRATCH = _decl()
SEMAPHORES = ["sV", "sS", "sP", "sG", "dx", "du", "dw", "dws", "dv", "arr0", "arr1", "arr2", "loc", "doy", "doa"]


def rank_program(g, core, T, topo):
    rank = T.rank_of(core)
    if rank is None:
        return
    nxt = T.cores[(rank + 1) % len(T.cores)]
    queue = {"V": g.vector, "S": g.scalar, "P": g.tensor, "G": g, "Y": g.sync}
    own = {"V": "sV", "S": "sS", "P": "sP", "G": "sG"}
    count = {}
    clock = {}
    known = {k: {} for k in queue}
    hist = {}

    def norm(a):
        if isinstance(a, str):
            a = (a, 0, 1 << 20)
        if a[0][:2] == "pb":
            return (a[0], 0, 1 << 20)
        return a

    def accesses(reads, writes):
        r = [norm(a) for a in reads]
        return [(a, "p" if a[0][:2] == "pb" else "r") for a in r] + [(norm(a), "w") for a in writes]

    def waits(q, acc):
        need = {}
        for (b, lo, hi), kind in acc:
            for e in hist.get(b, []):
                if e[0] >= hi or e[1] <= lo or (kind == "r" and e[2] == "r"):
                    continue
                if b[:2] == "pb" and kind == ("w" if e[2] == "w" else "p") and own.get(q) == e[3]:
                    continue
                need[e[3]] = max(need.get(e[3], 0), e[4])
        kn = known[q]
        for s in sorted(need, key=lambda s: -need[s]):
            if kn.get(s, 0) >= need[s]:
                continue
            queue[q].wait_ge(T.sem[s], need[s])
            for k, v in clock.get((s, need[s]), {}).items():
                kn[k] = max(kn.get(k, 0), v)
            kn[s] = max(kn.get(s, 0), need[s])

    def record(q, sem, n, acc):
        count[sem] = count.get(sem, 0) + n
        v = count[sem]
        clock[(sem, v)] = dict(known[q])
        for (b, lo, hi), kind in acc:
            h = hist.setdefault(b, [])
            if kind == "r":
                h[:] = [e for e in h if not (e[2] == "r" and e[3] == sem and e[0] >= lo and e[1] <= hi)]
            else:
                h[:] = [e for e in h if not (e[0] >= lo and e[1] <= hi)]
            h.append([lo, hi, kind, sem, v])

    def op(q, call, reads, writes):
        acc = accesses(reads, writes)
        waits(q, acc)
        call(queue[q]).then_inc(T.sem[own[q]], 1)
        record(q, own[q], 1, acc)

    def dma(q, out, in_, reads, writes, sem):
        acc = accesses(reads, writes)
        waits(q, acc)
        queue[q].dma_start(out, in_).then_inc(T.sem[sem], 16)
        record(q, sem, 16, acc)

    def V(call, reads, writes):
        op("V", call, reads, writes)

    def ts(out, in0, s1, s2, o0, o1, reads, writes):
        if o1 is None:
            V(lambda v: v.tensor_scalar(out, in0, s1, None, o0), reads, writes)
        else:
            V(lambda v: v.tensor_scalar(out, in0, s1, s2, o0, o1), reads, writes)

    def tt(out, a, b, o, reads, writes):
        V(lambda v: v.tensor_tensor(out, a, b, o), reads, writes)

    def fill(out, val, writes):
        V(lambda v: v.memset(out, val), [], writes)

    def act(out, in_, f, reads, writes, **kw):
        op("S", lambda s: s.activation(out, in_, f, **kw), reads, writes)

    def iota(out, pat, base, cm, writes, f=True):
        if f:
            op("G", lambda e: e.iota(out, pat, base, cm, allow_small_or_imprecise_dtypes=True), [], writes)
        else:
            op("G", lambda e: e.iota(out, pat, base, cm), [], writes)

    def quant(k, a, b, tile, lo, hi):
        qn, sn = "q" + k, "s" + k + "_p"
        V(lambda v: v.quantize_mx(T[qn][:, a:b], T[sn][:, a:b], T[tile][:, lo:hi]), [(tile, lo, hi)], [(qn, a, b), (sn, a, b)])

    def mm(bank, n, k, a, m, b, start=True, stop=True):
        qa, sa, qb, sq = "q" + k, "s" + k + "_p", "q" + m, "s" + m + "_p"
        op("P", lambda t: t.matmul_mx(T["pb%d" % bank][:, 0:n], T[qa][:, a:a + 128], T[sa][:, a:a + 128], T[qb][:, b:b + n], T[sq][:, b:b + n], start, stop),
           [(qa, a, a + 128), (sa, a, a + 128), (qb, b, b + n), (sq, b, b + n)], ["pb%d" % bank])

    def between(todo):
        if todo:
            todo.pop(0)()

    dma("Y", T.xt[:], T.x[:], [], ["xt"], "dx")
    dma("S", T.uv[:, 0:512], T.u[:], [], [("uv", 0, 512)], "du")
    dma("Y", T.qw[:].bitcast(dt.uint8), T.wc[:], [], ["qw"], "dw")
    dma("Y", T["sw_p"][:], T.ws[:], [], ["sw_p"], "dws")
    dma("Y", T.uv[:, 512:1024], T.v[:], [], [("uv", 512, 1024)], "dv")

    fill(T.zz[:], 0.0, ["zz"])
    fill(T.tg[:, 256:512], -1.0, [("tg", 256, 512)])
    iota(T.ci[:, 0:1], [[1, 1]], 0, 1, [("ci", 0, 1)], f=False)
    iota(T.ub[:, 0:8], [[16, 8]], 0, 0, ["ub"], f=False)
    iota(T.tg[:, 0:128], [[0, 4], [100, 2], [0, 16]], 0, 0, [("tg", 0, 128)])
    iota(T.tg[:, 128:256], [[0, 4], [100, 2], [0, 16]], -100, 0, [("tg", 128, 256)])
    for base, jj, code in ((256, 0, 8), (384, 1, 16)):
        iota(T.tg[:, base + jj:base + 128:32], [[1, 2], [0, 2]], code, 0, [("tg", base, base + 64)])
        iota(T.tg[:, base + jj + 2:base + 128:32], [[1, 4]], code, 0, [("tg", base + 64, base + 128)])
    iota(T.par[:], [[0, 10], [1, 2], [0, 16]], 0, 0, ["par"])
    iota(T.c0[:], [[64, 4], [1, 40]], -1, 0, ["c0"])
    for h in range(2):
        for k in range(2):
            lo = 512 + 128 * h + 64 * k
            iota(T.tg[:, lo:lo + 64], [[0, 2], [100, 2], [0, 16]], k - 100 * h, 0, [("tg", lo, lo + 64)])
    for h in range(2):
        lo = 768 + 128 * h
        iota(T.tg[:, lo:lo + 128], [[1, 4], [100, 2], [0, 16]], -100 * h, 0, [("tg", lo, lo + 128)])
    iota(T.tg[:, 1024:1152], [[1, 8], [0, 16]], 0, 0, [("tg", 1024, 1152)])
    fill(T.tg[:, 1152:1536], -1.0, [("tg", 1152, 1536)])
    for i, (base, jj, code) in enumerate(((1152, 0, 8), (1152, 1, 17), (1280, 0, 9), (1408, 1, 16))):
        iota(T.tg[:, base + jj:base + 128:32], [[2, 4]], code, 0, [("tg", 1152 + 96 * i, 1248 + 96 * i)])
    iota(T.ix[:, 0:128], [[1, 128]], 0, 0, [("ix", 0, 128)])
    iota(T.ix[:, 128:256], [[16, 4], [0, 2], [1, 16]], 0, 0, [("ix", 128, 256)])
    iota(T.ix[:, 128:144], [[1, 16]], 112, 0, [("ix", 128, 256)])
    iota(T.hrow[:], [[1, 8], [0, 40]], 0, 0, ["hrow"])
    iota(T.si0[:], [[1, 320]], 1, 0, ["si0"])
    iota(T.si1[:], [[1, 8], [8, 40]], 1, 0, ["si1"])
    iota(T.ccol[:], [[1, 320]], 0, 0, ["ccol"])
    iota(T.nx[:, 0:20], [[16, 20]], 0, 0, [("nx", 0, 20)], f=False)
    for n, w in (("ct", 512), ("fl", 352)):
        for b in range(4):
            act(T[n][:, w * b:w * b + w], T.zz[:, 0:w], AF.Copy, ["zz"], [(n, w * b, w * b + w)])

    def ci(i):
        return T.ci[:, i:i + 1]

    def cf(i):
        return T.cf[:, i:i + 1]

    def C(i):
        return ("ci", i, i + 1)

    def K(i):
        return ("cf", i, i + 1)
    RK, SG, HF, BK, GR = 1, 2, 3, 4, 5
    ts(ci(RK), ci(0), 15, None, O.bitwise_and, None, [C(0)], [C(RK)])
    ts(ci(GR), ci(0), 4, None, O.arith_shift_right, None, [C(0)], [C(GR)])
    ts(ci(SG), ci(0), 7, None, O.bitwise_and, None, [C(0)], [C(SG)])
    ts(ci(HF), ci(0), 16, 4, O.bitwise_and, O.arith_shift_right, [C(0)], [C(HF)])
    ts(ci(BK), ci(0), 5, None, O.arith_shift_right, None, [C(0)], [C(BK)])
    ts(cf(0), ci(RK), 3.0, None, O.is_ge, None, [C(RK)], [K(0)])
    ts(cf(1), ci(RK), 6.0, None, O.is_ge, None, [C(RK)], [K(1)])
    ts(cf(9), ci(RK), 9.0, 100.0, O.is_ge, O.mult, [C(RK)], [K(9)])
    tt(cf(2), cf(0), cf(1), O.add, [K(0), K(1)], [K(2)])
    tt(cf(10), cf(9), ci(GR), O.add, [K(9), C(GR)], [K(10)])
    ts(cf(3), cf(2), -3.0, None, O.mult, None, [K(2)], [K(3)])
    ts(cf(8), cf(2), 8.0, None, O.mult, None, [K(2)], [K(8)])
    ts(cf(13), cf(2), 2.0, HUGE, O.is_equal, O.mult, [K(2)], [K(13)])
    ts(cf(12), cf(2), 1.0, HUGE, O.is_equal, O.mult, [K(2)], [K(12)])
    tt(cf(4), cf(3), ci(RK), O.add, [K(3), C(RK)], [K(4)])
    tt(cf(11), cf(8), cf(10), O.add, [K(8), K(10)], [K(11)])
    tt(cf(14), cf(12), cf(13), O.subtract, [K(12), K(13)], [K(14)])
    ts(cf(5), cf(4), 1.0, 1.0, O.is_equal, O.add, [K(4)], [K(5)])
    ts(cf(6), cf(4), 0.0, 3.0, O.is_equal, O.mult, [K(4)], [K(6)])
    ts(T.ulist[:, 0:8], T.ub[:, 0:8], cf(4), None, O.add, None, ["ub", K(4)], ["ulist"])
    tt(cf(7), cf(5), cf(6), O.add, [K(5), K(6)], [K(7)])
    act(T.th[:], T.par[:], AF.Identity, ["par", K(14), K(13)], ["th"], scale=cf(14), bias=cf(13))
    for b in range(4):
        act(T.et[:, 512 * b:512 * b + 512], T.zz[:], AF.Copy, ["zz"], [("et", 512 * b, 512 * b + 512)])

    def conts(i, k):
        lo, hi = 512 * i, 512 * i + 512
        ts(T.ct[:, 0:2048:4], T.tg[:, lo:hi], cf(11), cf(7), O.is_equal, O.mult, [("tg", lo, hi), K(11), K(7)], ["ct"])
        quant(k, 0, 512, "ct", 0, 2048)
    conts(0, "a")
    quant("u", 0, 128, "uv", 0, 512)
    quant("0", 0, 320, "xt", 0, 1280)
    V(lambda v: v.tensor_copy(T.qup[:, 0:128].bitcast(dt.uint32), T.qu[:, 0:128].bitcast(dt.uint32).indirect(T.ulist[:, 0:8])), ["qu", "ulist"], ["qup"])
    V(lambda v: v.tensor_copy(T["sup_p"][:, 0:128], T["su_p"][:, 0:128].indirect(T.ulist[:, 0:8])), ["su_p", "ulist"], ["sup_p"])
    ts(cf(20), ci(SG), -BIG, None, O.mult, None, [C(SG)], [K(20)])
    ts(cf(21), ci(HF), 256.0, None, O.mult, None, [C(HF)], [K(21)])
    ts(cf(22), ci(HF), 16.0, None, O.mult, None, [C(HF)], [K(22)])
    ts(T.d0h[:], T.c0[:], cf(21), None, O.add, None, ["c0", K(21)], ["d0h"])
    ts(cf(23), ci(HF), 0.0, None, O.is_equal, None, [C(HF)], [K(23)])
    ts(cf(24), ci(HF), 1.0, None, O.is_equal, None, [C(HF)], [K(24)])
    V(lambda v: v.tensor_copy(T.c0[:], T.d0h[:]), ["d0h"], ["c0"])
    for i, (src, least) in enumerate(((BK, 2.0), (BK, 1.0), (GR, 1.0))):
        ts(cf(25 + 2 * i), ci(src), least, None, O.is_ge, None, [C(src)], [K(25 + 2 * i)])
        ts(cf(26 + 2 * i), ci(src), least, 8.0, O.is_lt, O.mult, [C(src)], [K(26 + 2 * i)])
    fill(T.top[:], 3.0e7, ["top"])
    for n in ("wt", "w8", "ft"):
        fill(T[n][:], 0, [n])
    UNITS = (("e", 0, 1.0), ("h", 128, 0.5), ("g", 0, 128.0))

    def unit(j):
        k, i, val = UNITS[j]
        for b in range(4):
            act(T.et[:, 512 * b + b:512 * b + 512:4], T.idx[:, i:i + 128], AF.Copy, [("idx", i, i + 128)], [("et", 512 * b, 512 * b + 512)], scale=val)

    def unit_done(j):
        quant(UNITS[j][0], 0, 512, "et", 0, 2048)
        if j < 2:
            unit(j + 1)

    def units():
        V(lambda v: v.tensor_copy(cf(40), ci(0)), [C(0)], [K(40)])
        for i in range(2):
            a, b = 128 * i, 128 * i + 128
            ts(T.idx[:, a:b], T.ix[:, a:b], cf(40), None, O.is_equal, None, [("ix", a, b), K(40)], [("idx", a, b)])
        unit(0)

    def scan(out, d0, d1, reads, writes):
        V(lambda v: v.tensor_tensor_scan(out, d0, d1, -4.0, O.max, O.add), reads, writes)

    def stage(st, todo):
        d0 = "c0"
        if st:
            o = 16 * st - 16
            d0 = "d0h"
            for a, b in ((0, 96), (96, 160)):
                tt(T.d0h[:, a:b], T.wt[:, 0:16].indirect(T.off12[:, o + a // 16:o + b // 16]), T.c0[:, a:b], O.add, ["wt", ("off12", o, o + 16), "c0"], [("d0h", a, b)])
        dn, an = "dst%d" % st, "ast%d" % st
        for h in range(4):
            a, b = 40 * h, 40 * h + 40
            scan(T.tt[:, a:b], T[d0][:, a:b], T[dn][:, a:b], [(d0, a, b), dn], [("tt", a, b)])
        for a, b in ((0, 80), (80, 160)):
            tt(T.vv[:, a:b], T.tt[:, a:b], T[an][:, a:b], O.max, [("tt", a, b), an], [("vv", a, b)])
        for i in range(2):
            V(lambda v: v.tensor_reduce(T.mcol[:, i:i + 1], T.vv[:, 80 * i:80 * i + 80], AxisListType.X, O.min), [("vv", 80 * i, 80 * i + 80)], [("mcol", i, i + 1)])
        between(todo)
        ts(T.mb[:], T.top[:], T.mcol[:, 0:1], T.mcol[:, 1:2], O.min, O.min, ["top", "mcol"], ["mb"])
        between(todo)
        V(lambda v: v.transpose(T.tb[:], T.mb[:]), ["mb"], ["tb"])
        between(todo)
        tt(T.mi[:, 0:8], T.tb[:, 0:8], T.tb[:, 16:24], O.min, ["tb"], ["mi"])
        between(todo)
        if st < 2:
            ts(T.wt[:, 0:8], T.mi[:, 0:8], 0xFFE00, None, O.bitwise_and, None, ["mi"], [("wt", 0, 8)])
        else:
            ts(T.w8[:, 0:8], T.mi[:, 0:8], 0xFFE00, 6, O.bitwise_and, O.arith_shift_right, ["mi"], [("w8", 0, 8)])
        while todo:
            between(todo)

    def lists(src, dst, at, j, n, mk):
        k = n // 2
        return [lambda e=e: ts(T[dst][:, at + e:at + n:2], T[src][:, j + e:16 * n:32], cf(mk), cf(mk + 1), O.mult, O.add, [src, K(mk), K(mk + 1)], [(dst, at + k * e, at + k * e + k)]) for e in range(2)]

    def symbols(part):
        sts = ()
        if part == 0:
            mm(2, 160, "a", 0, "f", 16, True, False)
            mm(2, 160, "a", 128, "f", 176, False, True)
            for i, (a, sh) in enumerate(((256, 0), (256, 144), (384, 16), (384, 160))):
                mm(3, 160, "a", a, "f", 16 + sh, i == 0, i == 3)
            sts = ((0, 2),)
        elif part == 1:
            for st in (1, 2):
                mm(3 + st, 160, "b", 256 * (st - 1), "f", 16, True, False)
                mm(3 + st, 160, "b", 256 * (st - 1) + 128, "f", 176, False, True)
            sts = ((1, 4), (2, 5))
        else:
            for i, (a, sh) in enumerate(((128, 0), (256, -16), (384, 16))):
                mm(7, 320, "c", a, "f", 16 + sh, i == 0, i == 2)
            mm(6, 320, "c", 0, "f", 16)
        for st, bank in sts:
            pb = "pb%d" % bank
            act(T["dst%d" % st][:], T[pb][:, 0:160], AF.Identity, [pb], ["dst%d" % st], scale=512.0, bias=513.0)
            act(T["ast%d" % st][:], T[pb][:, 0:160], AF.Abs, [pb, K(20)], ["ast%d" % st], scale=BIG, bias=cf(20))
        if part == 2:
            act(T.dow[:], T.pb6[:, 0:320], AF.Identity, ["pb6"], ["dow"], scale=8.0, bias=8.0)

    def decode(r):
        for i in range(8):
            k, dst, b = ("e", "fp", i) if i < 4 else ("h", "f2", i - 4)
            bank = i % 2
            mm(bank, 320, k, 128 * b, str(r), 0)
            act(T[dst][:, 320 * b:320 * b + 320], T["pb%d" % bank][:, 0:320], AF.Copy, ["pb%d" % bank], [(dst, 320 * b, 320 * b + 320)])

    def first_table(r):
        ca, cb = (1.0, 40.0) if r == 0 else (8.0, 1.0)

        def X(i):
            return T.fx[:, 16 * i:16 * i + 8]

        def F(i):
            return ("fx", 16 * i, 16 * i + 8)
        m = T.mi[:, 0:8]
        return [lambda: ts(X(0), m, 63, None, O.bitwise_and, None, ["mi"], [F(0)]),
                lambda: ts(X(1), m, 448, 6, O.bitwise_and, O.arith_shift_right, ["mi"], [F(1)]),
                lambda: ts(X(2), X(0), ca, 1.0, O.mult, O.add, [F(0)], [F(2)]),
                lambda: ts(X(5), X(1), cb, None, O.mult, None, [F(1)], [F(5)]),
                lambda: ts(X(4), m, BIG, 512.0, O.is_lt, O.mult, ["mi"], [F(4)]),
                lambda: tt(X(3), X(2), X(5), O.add, [F(2), F(5)], [F(3)]),
                lambda: tt(T.ft[:, 0:8], X(3), X(4), O.mult, [F(3), F(4)], [("ft", 0, 8)])]

    def order(r):
        todo = first_table(r)
        for a in (0, 160):
            tt(T.d0o[:, a:a + 160], T.w8[:, 0:16].indirect(T.offd[:, a // 16:a // 16 + 10]), T.hrow[:, a:a + 160], O.add, ["w8", "offd", "hrow"], [("d0o", a, a + 160)])
        for h in range(8):
            a, b = 40 * h, 40 * h + 40
            scan(T.kap[:, 16 + a:16 + b], T.d0o[:, a:b], T.dow[:, a:b], [("d0o", a, b), "dow"], [("kap", 16 + a, 16 + b)])
        for a in (0, 160):
            V(lambda v: v.transpose(T.kt[:, a:a + 160], T.kap[:, 16 + a:176 + a]), [("kap", 16 + a, 176 + a)], [("kt", a, a + 160)])
        V(lambda v: v.transpose(T.kt[:, 320:672], T.kap[:]), ["kap"], [("kt", 320, 672)])
        between(todo)
        between(todo)
        ts(T.ex[:, 0:21], T.kt[:, 0:672:32], cf(23), None, O.mult, None, ["kt", K(23)], [("ex", 0, 21)])
        ts(T.ex[:, 24:45], T.kt[:, 16:672:32], cf(24), None, O.mult, None, ["kt", K(24)], [("ex", 24, 45)])
        between(todo)
        tt(T.my[:, 0:10], T.ex[:, 0:10], T.ex[:, 34:44], O.add, ["ex"], [("my", 0, 10)])
        tt(T.my[:, 10:20], T.ex[:, 11:21], T.ex[:, 24:34], O.add, ["ex"], [("my", 10, 20)])
        for q in range(NS):
            a = 320 * (q % 2)
            act(T.sj[:, a:a + 320], T.kap[:, 16:336], AF.Sign, [("kap", 16, 336), ("my", q, q + 1)], [("sj", a, a + 320), ("acc", q, q + 1)], scale=-1.0, bias=T.my[:, q:q + 1], accum_out=T.acc[:, q:q + 1])
        V(lambda v: v.tensor_copy(T.ku[:], T.kap[:, 16:336]), [("kap", 16, 336)], ["ku"])
        between(todo)

        def less(p):
            a = 320 * (p % 3)
            ts(T.fab[:, a:a + 320], T.ku[:], T.my[:, NS + p:NS + p + 1], None, O.is_lt, None, ["ku", ("my", NS + p, NS + p + 1)], [("fab", a, a + 320)])
        less(0)
        for p in range(NV):
            if p + 1 < NV:
                less(p + 1)
            a, lo = 320 * (p % 3), 160 * p
            V(lambda v: v.tensor_tensor_scan(T.scn[:, lo:lo + 160], T.fab[:, a:a + 160], T.fab[:, a + 160:a + 320], -160.0, O.add, O.add), [("fab", a, a + 320)], [("scn", lo, lo + 160)])
            between(todo)
        si = "si0" if r == 0 else "si1"
        tt(T.vrow[:], T.ft[:, 0:16].indirect(T.offd[:, 0:20]), T[si][:], O.add, ["ft", "offd", si], ["vrow"])
        for src, n, a, b, m, c in (("scn", slice(159, 160 * NV, 160), NS, 20, 0.0625, 10.0), ("acc", slice(0, NS), 0, NS, 0.03125, 9.96875)):
            ts(T.rf[:, a:b], T[src][:, n], m, c, O.mult, O.add, [src], [("rf", a, b)])
            ts(T.rx[:, a:b], T[src][:, n], m, c - 0.46875, O.mult, O.add, [src], [("rx", a, b)])
        tt(T.rf[:, 32:52], T.rf[:, 0:20], T.rx[:, 0:20], O.add, [("rf", 0, 20), ("rx", 0, 20)], [("rf", 32, 52)])
        for e in range(2):
            ts(T.offs[:, e:20:2], T.rf[:, 32 + 10 * e:42 + 10 * e], 16.0, cf(22), O.mult, O.add, [("rf", 32, 52), K(22)], [("offs", 10 * e, 10 * e + 10)])
        V(lambda v: v.tensor_copy(T.win[:, 0:640].indirect(T.offs[:, 0:20]), T.vrow[:]), ["vrow", "offs"], ["win"])

    def L(i):
        return T.lx[:, 16 * i:16 * i + 10]

    def LR(i):
        return ("lx", 16 * i, 16 * i + 10)

    def plane(n, b):
        return (n, 320 * b, 320 * b + 320)

    def laid(r):
        V(lambda v: v.transpose(T.tw[:, 0:320], T.win[:, 0:320]), [("win", 0, 320)], [("tw", 0, 320)])
        tt(L(0), T.tw[:, 0:320:32], T.tw[:, 16:320:32], O.add, [("tw", 0, 320)], [LR(0)])
        ts(L(1), L(0), 511, None, O.bitwise_and, None, [LR(0)], [LR(1)])
        ts(L(3), L(0), 512.0, None, O.is_lt, None, [LR(0)], [LR(3)])
        ts(L(2), L(0), 9, None, O.arith_shift_right, None, [LR(0)], [LR(2)])
        ts(T.ll[:, 0:10], L(1), -1.0, None, O.add, None, [LR(1)], ["ll"])
        for b in range(4):
            act(T.pz[:, 160 * b:160 * b + 160], T.fp[:, 320 * b:320 * b + 320].indirect(T.ll[:, 0:10]), AF.Copy, [plane("fp", b), "ll"], [("pz", 160 * b, 160 * b + 160)], scale=0.5)
        tt(L(4), L(3), L(1), O.mult, [LR(3), LR(1)], [LR(4)])
        tt(L(5), L(4), L(2), O.add, [LR(4), LR(2)], [LR(5)])
        ts(T.bl[:, 0:10], L(5), -1.0, None, O.add, None, [LR(5)], ["bl"])
        for b in range(4):
            tt(T.zt[:, b:640:4], T.f2[:, 320 * b:320 * b + 320].indirect(T.bl[:, 0:10]), T.pz[:, 160 * b:160 * b + 160], O.add,
               [plane("f2", b), "bl", ("pz", 160 * b, 160 * b + 160)], [("zt", 160 * b, 160 * b + 160)])
        z, l = "z%d" % r, "l%d" % r
        quant(z, 0, 160, "zt", 0, 640)
        rid, pid, _ = topo.addr(nxt)
        m = topo.mask(core, nxt)
        arr = "arr%d" % r
        waits("G", accesses(["q" + z, "s" + z + "_p"], []))
        g.remote_dma(T["q" + l][:, 0:160].bitcast(dt.uint8), T["q" + z][:, 0:160].bitcast(dt.uint8), T.sem[arr], T.sem["loc"], pid, rid, m)
        g.remote_dma(T["s" + l + "_p"][:, 0:160], T["s" + z + "_p"][:, 0:160], T.sem[arr], T.sem["loc"], pid, rid, m)
        k = 2 * len(topo.engines(core, nxt))
        count["loc"] = count.get("loc", 0) + k
        count[arr] = k
        for n in ("q" + l, "s" + l + "_p"):
            hist[n] = [[0, 160, "w", arr, k]]

    def kept(r):
        V(lambda v: v.transpose(T.tw[:, 320:640], T.win[:, 320:640]), [("win", 320, 640)], [("tw", 320, 640)])
        tt(L(6), T.tw[:, 320:640:32], T.tw[:, 336:640:32], O.add, [("tw", 320, 640)], [LR(6)])
        ts(L(7), L(6), 511, None, O.bitwise_and, None, [LR(6)], [LR(7)])
        ts(T.kl[:, 0:10], L(7), -1.0, None, O.add, None, [LR(7)], ["kl"])
        for b in range(4):
            rd, wr = [plane("fp", b), "kl"], [("xk", 160 * b, 160 * b + 160)]
            if b % 2:
                act(T.xk[:, b:640:4], T.fp[:, 320 * b:320 * b + 320].indirect(T.kl[:, 0:10]), AF.Copy, rd, wr)
            else:
                V(lambda v: v.tensor_copy(T.xk[:, b:640:4], T.fp[:, 320 * b:320 * b + 320].indirect(T.kl[:, 0:10])), rd, wr)
        quant(str(r + 1), 0, 160, "xk", 0, 640)

    def arrive(r):
        for b in range(4):
            mm(2 + b, 160, "w", 128 * b, "l%d" % r, 0, True, False)
            mm(2 + b, 160, "g", 128 * b, "l%d" % r, 0, False, True)
        for b in range(4):
            pb, wr = "pb%d" % (2 + b), [("xh", 160 * b, 160 * b + 160)]
            if b % 2:
                ts(T.xh[:, b:640:4], T[pb][:, 0:160], 0.0078125, None, O.mult, None, [pb], wr)
            else:
                act(T.xh[:, b:640:4], T[pb][:, 0:160], AF.Copy, [pb], wr, scale=0.0078125)
        quant(str(r + 1), 160, 320, "xh", 0, 640)

    def product_v(half):
        mm(half, 160, "v", 0, "3", 160 * half)
        for h in range(8):
            a = 40 * h + 20 * half
            act(T.yo[:, a:a + 20], T["pb%d" % half][:, h:160:8], AF.Copy, ["pb%d" % half], [("yo", a, a + 20)])

    def flags(half, bank):
        for h in range(8):
            a = 40 * h + 20 * half
            tt(T.fl[:, 64 + 4 * a:144 + 4 * a:4], T["pb%d" % bank][:, h:160:8], T.th[:, a:a + 20], O.is_gt, ["pb%d" % bank, "th"], [("fl", 64 + 4 * a, 144 + 4 * a)])

    for r in range(3):
        if r == 0:
            mm(0, 320, "up", 0, "0", 0)
            for a in (0, 160):
                tt(T.fl[:, 64 + 4 * a:704 + 4 * a:4], T.pb0[:, a:a + 160], T.th[:, a:a + 160], O.is_gt, ["pb0", "th"], [("fl", 64 + 4 * a, 704 + 4 * a)])
        else:
            mm(1, 160, "up", 0, str(r), 160)
            flags(1, 1)
        quant("f", 0, 176, "fl", 0, 704)
        quant("f", 176, 352, "fl", 704, 1408)
        symbols(0)
        half = [lambda: V(lambda v: v.transpose(T.tl[:], T.pb3[:, 0:160]), ["pb3"], ["tl"])] + lists("tl", "off12", 0, 0, 10, 25) + lists("tl", "off12", 16, 2, 10, 27)
        full = [lambda: V(lambda v: v.transpose(T.tlo[:], T.pb7[:, 0:320]), ["pb7"], ["tlo"])] + lists("tlo", "offd", 0, 0, 20, 29)
        if r == 0:
            conts(1, "b")
            symbols(1)
            stage(0, half + [lambda: conts(2, "c"), units])
            symbols(2)
            stage(1, [lambda: fill(T.kap[:], 0.0, ["kap"]), lambda: unit_done(0), lambda: fill(T.win[:], 0.0, ["win"]), lambda: unit_done(1)])
            unit_done(2)
            decode(r)
        else:
            symbols(1)
            symbols(2)
            decode(r)
            stage(0, half)
            stage(1, [])
        stage(2, full)
        order(r)
        laid(r)
        kept(r)
        if r < 2:
            mm(0, 160, "up", 0, str(r + 1), 0)
            flags(0, 0)
        else:
            quant("v", 0, 128, "uv", 512, 1024)
            product_v(0)
            for e in range(2):
                ts(T.offo[:, e:20:2], T.rf[:, 10 * e:10 * e + 10], 16.0, None, O.mult, None, [("rf", 0, 20)], [("offo", 10 * e, 10 * e + 10)])
            V(lambda v: v.tensor_copy(T.oprow[:, 0:320].indirect(T.offo[:, 0:20]), T.ccol[:]), ["ccol", "offo"], ["oprow"])
            for k in range(8):
                dma("Y", T.op[k:k + 1, :], T.oprow[16 * k:16 * k + 1, :], ["oprow"], [], "doy")

            def N(i):
                return T.nx[:, 20 * i:20 * i + 20]

            def NR(i):
                return ("nx", 20 * i, 20 * i + 20)
            V(lambda v: v.tensor_copy(cf(41), ci(RK)), [C(RK)], [K(41)])
            ts(N(1), N(0), cf(41), None, O.add, None, [NR(0), K(41)], [NR(1)])
            ts(N(0), N(1), 205.0, None, O.mult, None, [NR(1)], [NR(0)])
            ts(N(2), N(0), 13, None, O.arith_shift_right, None, [NR(0)], [NR(2)])
            ts(N(0), N(2), -319.0, None, O.mult, None, [NR(2)], [NR(0)])
            ts(N(2), N(1), 8.0, None, O.mult, None, [NR(1)], [NR(2)])
            tt(T.fx[:, 96:116], N(0), N(2), O.add, [NR(0), NR(2)], [("fx", 96, 116)])
            V(lambda v: v.tensor_copy(T.nat[:, 0:20], T.fx[:, 96:116]), [("fx", 96, 116)], ["nat"])
        arrive(r)
    product_v(1)
    dma("S", T.y[:], T.yo[:], ["yo"], [], "doa")
    V(lambda v: v.tensor_copy(T["sn_p"][:, 0:320], T["s3_p"][:, 0:320].indirect(T.nat[:, 0:20])), ["s3_p", "nat"], ["sn_p"])
    for k in range(4):
        dma("S" if k % 2 else "Y", T.osc[4 * k:4 * k + 4, :], T["sn_p"][32 * k:32 * k + 4, :], ["sn_p"], [], "doa" if k % 2 else "doy")
    V(lambda v: v.tensor_copy(T.qn[:, 0:320].bitcast(dt.uint32), T.q3[:, 0:320].bitcast(dt.uint32).indirect(T.nat[:, 0:20])), ["q3", "nat"], ["qn"])
    dma("Y", T.oc[:], T.qn[:].bitcast(dt.uint8), ["qn"], [], "doy")
    for s in sorted(count):
        if known["G"].get(s, 0) < count[s]:
            g.wait_ge(T.sem[s], count[s])
